import numpy as np
import ml_dtypes


def mxq(x, axis, fmt="e4m3"):
    dtype, down = {"e4m3": (ml_dtypes.float8_e4m3fn, 7), "e5m2": (ml_dtypes.float8_e5m2, 14)}[fmt]
    v = np.moveaxis(np.asarray(x, np.float32).astype(ml_dtypes.bfloat16).astype(np.float64), axis, -1)
    blocks = v.reshape(v.shape[:-1] + (-1, 32))
    amax = np.abs(blocks).max(-1, keepdims=True)
    byte = np.maximum(np.where(amax > 0, np.frexp(amax)[1] - 1 + 127, 0) - down, 1)
    scale = np.exp2(byte - 127.0)
    codes = (blocks / scale).astype(np.float32).astype(dtype).astype(np.float64)
    return np.moveaxis((codes * scale).reshape(v.shape), -1, axis)


WIDE = False


def mx_kscale(k):
    if not WIDE:
        return np.ones(k)
    levels = np.array([10, -10, 5, -5, 0])
    if k % 512:
        return np.exp2(np.random.permutation(np.resize(levels, k // 32))).repeat(32)
    a = np.empty((k // 512, 16))
    for p in range(k // 512):
        a[p, :8] = np.random.permutation(np.resize(levels, 8))
        for g in range(8):
            far = levels[np.abs(levels - a[p, g]) >= 10]
            a[p, g + 8] = far[np.random.randint(len(far))]
    return np.exp2(a.ravel()).repeat(32)


def f64(x):
    return np.asarray(x).astype(np.float64)


def striped(idx):
    return np.tile(idx.reshape(-1, 16).T, (8, 1)).astype(np.uint16)


def unstriped(offs):
    return offs[:16].T.reshape(-1).astype(np.int64)


E2M1 = np.array([0.0, 0.5, 1.0, 1.5, 2.0, 3.0, 4.0, 6.0, -0.0, -0.5, -1.0, -1.5, -2.0, -3.0, -4.0, -6.0])


def pack_weight(w, fmt):
    k, n = w.shape
    w = f64(np.asarray(w, np.float32).astype(ml_dtypes.bfloat16)).reshape(k // 32, 32, n)
    amax = np.abs(w).max(1)
    if fmt == "e4m3":
        byte = np.frexp(amax)[1] - 1 + 127 - 7
    else:
        mant, ex = np.frexp(amax / 6.0)
        byte = np.where(mant > 0.5, ex, ex - 1) + 127
    byte = np.clip(np.where(amax > 0, byte, 1), 1, 254)
    scaled = (w * np.exp2(127.0 - byte)[:, None, :]).reshape(k, n).astype(np.float32)
    by_word = np.ascontiguousarray(scaled.reshape(k // 512, 128, 4, n).transpose(0, 1, 3, 2))
    if fmt == "e4m3":
        words = by_word.astype(ml_dtypes.float8_e4m3fn).view(np.uint8)
    else:
        c = by_word.astype(ml_dtypes.float4_e2m1fn).view(np.uint8) & 0xF
        words = (c[..., 0::2] | (c[..., 1::2] << 4)).reshape(k // 512, 128, 2 * n)
    return np.ascontiguousarray(words), np.ascontiguousarray(byte.astype(np.uint8).reshape(k // 512, 16, n))


def unpack_weight(words, scales, fmt):
    g, _, n = scales.shape
    words = np.ascontiguousarray(words).reshape(g, 128, n, -1)
    if fmt == "e4m3":
        vals = words.view(ml_dtypes.float8_e4m3fn).astype(np.float64)
    else:
        nib = np.empty((g, 128, n, 4), np.uint8)
        nib[..., 0::2] = words & 0xF
        nib[..., 1::2] = words >> 4
        vals = E2M1[nib]
    vals = vals * np.repeat(np.exp2(scales.astype(np.float64) - 127.0), 8, axis=1)[..., None]
    return vals.transpose(0, 1, 3, 2).reshape(g * 512, n)


def gelu(v):
    return 0.5 * v * (1.0 + np.tanh(np.sqrt(2.0 / np.pi) * (v + 0.044715 * v**3)))


K, T, S, M, N = 1024, 2048, 1024, 1024, 512

def setup_inputs():
    n = np.random.standard_normal
    s = mx_kscale(K)[:, None]
    u = mx_kscale(S)[:, None]
    idx = np.random.permutation(T)[:S]
    tab_words, tab_scales = pack_weight(n((K, T)) * s / np.sqrt(K), "e4m3")
    wf_words, wf_scales = pack_weight(0.6 * n((K, N)) * s / np.sqrt(K), "e2m1")
    wdT = n((N, T)) / np.sqrt(S)
    wdT[:, idx] /= u.T
    return {
        "x": (n((K, M)) / s).astype(np.float32),
        "tab_words": tab_words, "tab_scales": tab_scales,
        "offs": striped(idx),
        "r": (0.6 * n((S, M))).astype(np.float32),
        "g": (np.exp(0.3 * n(S)) * u[:, 0]).astype(np.float32),
        "wdT": wdT.astype(np.float32),
        "wf_words": wf_words, "wf_scales": wf_scales,
        "c": (0.4 * n(N)).astype(np.float32),
    }

def reference(x, tab_words, tab_scales, offs, r, g, wdT, wf_words, wf_scales, c):
    v = unpack_weight(tab_words, tab_scales, "e4m3")[:, unstriped(offs)]
    wd = f64(wdT)[:, unstriped(offs)]
    wf = unpack_weight(wf_words, wf_scales, "e2m1")
    xq = mxq(f64(x), 0, "e4m3")
    p = v.T @ xq
    h = np.tanh(p + f64(r)) * f64(g)[:, None]
    y = mxq(wd, 1, "e4m3") @ mxq(h, 0, "e4m3") + wf.T @ xq
    return np.tanh(y + f64(c)[:, None])

@@ -1,0 +1,328 @@
+from contextlib import ExitStack
+
+import concourse.mybir as mybir
+from concourse.masks import make_identity
+
+K, T, S, M, N = 1024, 2048, 1024, 1024, 512
+FLOPS = 2 * S * K * M + 2 * N * S * M + 2 * N * K * M
+
+F32 = mybir.dt.float32
+BF16 = mybir.dt.bfloat16
+I32 = mybir.dt.int32
+U32 = mybir.dt.uint32
+U16 = mybir.dt.uint16
+U8 = mybir.dt.uint8
+FP8X4 = mybir.dt.float8_e4m3fn_x4
+FP4X4 = mybir.dt.float4_e2m1fn_x4
+ACT = mybir.ActivationFunctionType
+ALU = mybir.AluOpType
+
+P = 128
+PACK = 4
+PASS = P * PACK
+BANK = 512
+HALF = 512
+
+
+def tile_list_sparse_reservoir_control_kernel(tc, x, tab_words, tab_scales, offs, r, g, wdT, wf_words, wf_scales, c, out):
+    nc = tc.nc
+    with ExitStack() as ctx:
+        keep = ctx.enter_context(tc.tile_pool(name="keep", bufs=1))
+        ring = ctx.enter_context(tc.tile_pool(name="ring", bufs=3))
+        psum_p = ctx.enter_context(tc.psum_pool(name="psum_p", bufs=3))
+        psum_y = ctx.enter_context(tc.psum_pool(name="psum_y", bufs=5))
+
+        offsets = keep.tile([P, S // 16], U16, name="offsets")
+        nc.sync.dma_start(offsets[:], offs)
+
+        tab_plane = keep.tile([P, T // 4], I32, name="tab_plane", align_bytes=64)
+        nc.vector.memset(tab_plane[:], 0)
+        wf_plane = keep.tile([P, 2, N // 4], I32, name="wf_plane", align_bytes=64)
+        nc.vector.memset(wf_plane[:], 0)
+        warm = keep.tile([P, 8], F32, name="warm")
+        nc.vector.memset(warm[:], 0.0)
+        for q in range(4):
+            nc.sync.dma_start(tab_plane[32 * q : 32 * q + 8, :], tab_scales[:, 4 * q : 4 * q + 4, :].bitcast(I32))
+        warm_out = keep.tile([P, 8], F32, name="warm_out")
+        nc.scalar.activation(warm_out[:], warm[:], ACT.Tanh)
+
+        tab = [keep.tile([P, T], I32, name=f"tab{a}", align_bytes=64) for a in range(2)]
+        wd_raw = [keep.tile([P, T], F32, name=f"wd_raw{i}", align_bytes=64) for i in range(N // P)]
+        wf = keep.tile([P, 2, 2 * N // 4], I32, name="wf", align_bytes=64)
+        g_sb = keep.tile([P, 2, PACK], F32, name="g_sb")
+        c_sb = keep.tile([P, N // P], F32, name="c_sb")
+        x_raw = keep.tile([P, 2, PACK, M], F32, name="x_raw", align_bytes=64)
+        r_sb = keep.tile([P, 2, PACK, M], F32, name="r_sb", align_bytes=64)
+
+        def load_tab(a):
+            nc.sync.dma_start(tab[a][:], tab_words[a].rearrange("p t i -> p (t i)").bitcast(I32))
+
+        def load_rows(dst, src, a, m0, w):
+            rows = src[a * PASS : (a + 1) * PASS, m0 : m0 + w]
+            nc.sync.dma_start(dst[:, a, :, m0 : m0 + w], rows.rearrange("(p t) m -> p t m", t=PACK))
+
+        def load_wd(i):
+            nc.sync.dma_start(wd_raw[i][:], wdT[i * P : (i + 1) * P, :])
+
+        def load_small():
+            nc.sync.dma_start(wf[:], wf_words.bitcast(I32).rearrange("a p e -> p a e"))
+            for row in range(4):
+                nc.sync.dma_start(wf_plane[row:P:32, :, :], wf_scales.bitcast(I32)[:, row:16:4, :].rearrange("a q e -> q a e"))
+            with nc.allow_non_contiguous_dma(reason="one bias a partition"):
+                nc.sync.dma_start(c_sb[:], c.rearrange("(i p) -> p i", p=P))
+
+        def load_g():
+            nc.sync.dma_start(g_sb[:], g.rearrange("(b p t) -> p b t", b=2, t=PACK))
+
+        load_tab(0)
+        load_tab(1)
+        load_rows(x_raw, x, 0, 0, 256)
+        load_rows(x_raw, x, 1, 0, 256)
+        load_g()
+        load_rows(r_sb, r, 0, 0, 256)
+        load_rows(r_sb, r, 1, 0, 256)
+        load_rows(x_raw, x, 0, 256, 256)
+        load_rows(x_raw, x, 1, 256, 256)
+        load_wd(0)
+        load_rows(r_sb, r, 0, 256, 256)
+        load_rows(r_sb, r, 1, 256, 256)
+        load_wd(1)
+        load_small()
+        load_rows(x_raw, x, 0, 512, 512)
+        load_rows(x_raw, x, 1, 512, 512)
+        load_wd(2)
+        load_wd(3)
+        load_rows(r_sb, r, 0, 512, 512)
+        load_rows(r_sb, r, 1, 512, 512)
+
+        ident = keep.tile([P, P], F32, name="ident", align_bytes=64)
+        make_identity(nc, ident[:])
+
+        v_codes = [keep.tile([P, S], U32, name=f"v_codes{a}", align_bytes=64) for a in range(2)]
+        v_plane_list = keep.tile([P, S], U8, name="v_plane_list", align_bytes=64)
+        v_plane = keep.tile([P, S], U8, name="v_plane", align_bytes=64)
+
+        def gather_tab(a):
+            nc.vector.tensor_copy(
+                v_codes[a][:].rearrange("k (b t p) -> k b p t", b=2, t=PACK),
+                tab[a][:].bitcast(U32).indirect(offsets[:]),
+            )
+
+        def gather_scales():
+            nc.vector.tensor_copy(v_plane_list[:], tab_plane[:].bitcast(U8).indirect(offsets[:]))
+
+        def turn_scales():
+            nc.vector.tensor_copy(
+                v_plane[:].rearrange("k (b t p) -> k b p t", b=2, t=PACK),
+                v_plane_list[:].rearrange("k (b p t) -> k b p t", b=2, t=PACK),
+            )
+
+        x_codes = keep.tile([P, 2, M], U32, name="x_codes", align_bytes=64)
+        x_plane = keep.tile([P, 2, M], U8, name="x_plane", align_bytes=64)
+        h_codes = keep.tile([P, 2, M], U32, name="h_codes", align_bytes=64)
+        h_plane = keep.tile([P, 2, M], U8, name="h_plane", align_bytes=64)
+        wd_codes = keep.tile([P, N // P, 2 * P], U32, name="wd_codes", align_bytes=64)
+        wd_plane = keep.tile([P, N // P, 2 * P], U8, name="wd_plane", align_bytes=64)
+        x_grouped = keep.tile([P, 2, M, PACK], BF16, name="x_grouped", align_bytes=64)
+        staged = {}
+
+        def group_x(engine, a, m0, w):
+            dst = x_grouped[:, a, m0 : m0 + w, :].rearrange("p (c i) t -> p c t i", i=4)
+            src = x_raw[:, a, :, m0 : m0 + w].rearrange("p t (c i) -> p c t i", i=4)
+            if engine == "S":
+                nc.scalar.copy(dst, src)
+            elif engine == "G":
+                nc.gpsimd.tensor_copy(dst, src)
+            else:
+                nc.vector.tensor_copy(dst, src)
+
+        def quantize_x(a, m0, w):
+            cols = slice(m0, m0 + w)
+            nc.vector.quantize_mx(
+                out=x_codes[:, a, cols].bitcast(FP8X4),
+                scales=x_plane[:, a, cols],
+                in_=x_grouped[:, a, cols, :].rearrange("p m t -> p (m t)"),
+            )
+
+        def make_h(b, m0, w, mode):
+            cols = slice(m0, m0 + w)
+            per_bank = BANK // w
+            z = ring.tile([P, PACK, w], F32, name="z", align_bytes=64)
+            for t0 in range(0, PACK, per_bank):
+                bank = psum_p.tile([P, per_bank, w], F32, name="p_bank")
+                for t in range(t0, t0 + per_bank):
+                    jcols = slice(b * PASS + t * P, b * PASS + (t + 1) * P)
+                    for a in range(2):
+                        nc.tensor.matmul_mx(
+                            out=bank[:, t - t0, :],
+                            lhsT=v_codes[a][:, jcols].bitcast(FP8X4),
+                            lhsT_scale=v_plane[4 * a : P, jcols],
+                            rhs=x_codes[:, a, cols].bitcast(FP8X4),
+                            rhs_scale=x_plane[:, a, cols],
+                            start=(a == 0),
+                            stop=(a == 1),
+                        )
+                nc.vector.tensor_tensor(z[:, t0 : t0 + per_bank, :], bank[:], r_sb[:, b, t0 : t0 + per_bank, cols], ALU.add)
+            hb = ring.tile([P, w, PACK], BF16, name="hb", align_bytes=64, bufs=3)
+            if mode == "S":
+                th = ring.tile([P, PACK, w], F32, name="th", align_bytes=64)
+                nc.scalar.activation(th[:], z[:], ACT.Tanh)
+                slots = ring.tile([P, PACK, w], BF16, name="slots", align_bytes=64)
+                for t in range(PACK):
+                    nc.scalar.activation(slots[:, t, :], th[:, t, :], ACT.Copy, scale=g_sb[:, b, t : t + 1])
+                staged[(b, m0)] = (slots, hb, mode, w)
+            else:
+                th = ring.tile([P, w, PACK], F32, name="th", align_bytes=64)
+                nc.scalar.activation(
+                    th[:].rearrange("p (c i) t -> p c t i", i=4),
+                    z[:].rearrange("p t (c i) -> p c t i", i=4),
+                    ACT.Tanh,
+                )
+                staged[(b, m0)] = (th, hb, mode, w)
+
+        def gain_h(b, m0):
+            th, hb, mode, w = staged[(b, m0)]
+            if mode == "S":
+                nc.vector.tensor_copy(hb[:].rearrange("p (c i) t -> p c t i", i=4), th[:].rearrange("p t (c i) -> p c t i", i=4))
+            elif mode == "G":
+                nc.gpsimd.tensor_tensor(hb[:], th[:], g_sb[:, b : b + 1, :].to_broadcast([P, w, PACK]), ALU.mult)
+            else:
+                nc.vector.tensor_tensor(hb[:], th[:], g_sb[:, b : b + 1, :].to_broadcast([P, w, PACK]), ALU.mult)
+
+        def quantize_h(b, m0):
+            th, hb, mode, w = staged[(b, m0)]
+            cols = slice(m0, m0 + w)
+            nc.vector.quantize_mx(
+                out=h_codes[:, b, cols].bitcast(FP8X4),
+                scales=h_plane[:, b, cols],
+                in_=hb[:].rearrange("p m t -> p (m t)"),
+            )
+
+        picked = [keep.tile([P, S], BF16, name=f"wd_picked{i}", align_bytes=64) for i in range(N // P)]
+        wd_grouped = [keep.tile([P, S], BF16, name=f"wd_grouped{i}", align_bytes=64) for i in range(N // P)]
+
+        def gather_wd(i, b):
+            nc.vector.tensor_copy(
+                picked[i][:, b * PASS : (b + 1) * PASS].rearrange("n (u p e) -> n p u e", u=2, e=2),
+                wd_raw[i][:].indirect(offsets[:, 32 * b : 32 * (b + 1)]),
+            )
+
+        def turn_wd(i):
+            words = picked[i][:].bitcast(F32)
+            turned = psum_y.tile([P, 4, P], F32, name="y_bank")
+            for s in range(4):
+                nc.tensor.transpose(turned[:, s, :], words[:, s * P : (s + 1) * P], ident[:])
+            nc.scalar.copy(
+                wd_grouped[i][:].bitcast(F32).rearrange("p (b n u) -> p b n u", b=2, u=2),
+                turned[:].rearrange("p (b u) n -> p b n u", b=2),
+            )
+
+        def quantize_wd(i):
+            nc.vector.quantize_mx(out=wd_codes[:, i, :].bitcast(FP8X4), scales=wd_plane[:, i, :], in_=wd_grouped[i][:])
+
+        def make_y(i, m0, w, groups, result=None):
+            bank = psum_y.tile([P, groups, w], F32, name="y_bank")
+            for s in range(groups):
+                cols = slice(m0 + s * w, m0 + (s + 1) * w)
+                for a in range(2):
+                    nc.tensor.matmul_mx(
+                        out=bank[:, s, :],
+                        lhsT=wf[:, a, :].bitcast(U8)[:, 2 * i * P : 2 * (i + 1) * P].bitcast(FP4X4),
+                        lhsT_scale=wf_plane[:, a, :].bitcast(U8)[:, i * P : (i + 1) * P],
+                        rhs=x_codes[:, a, cols].bitcast(FP8X4),
+                        rhs_scale=x_plane[:, a, cols],
+                        start=(a == 0),
+                        stop=False,
+                    )
+                for b in range(2):
+                    nc.tensor.matmul_mx(
+                        out=bank[:, s, :],
+                        lhsT=wd_codes[:, i, b * P : (b + 1) * P].bitcast(FP8X4),
+                        lhsT_scale=wd_plane[:, i, b * P : (b + 1) * P],
+                        rhs=h_codes[:, b, cols].bitcast(FP8X4),
+                        rhs_scale=h_plane[:, b, cols],
+                        start=False,
+                        stop=(b == 1),
+                    )
+            if result is None:
+                result = ring.tile([P, groups * w], F32, name="result", align_bytes=64, bufs=4)
+                nc.scalar.activation(result[:], bank[:].rearrange("p s w -> p (s w)"), ACT.Tanh, bias=c_sb[:, i : i + 1])
+                nc.sync.dma_start(out[i * P : (i + 1) * P, m0 : m0 + groups * w], result[:])
+            else:
+                nc.scalar.activation(result[:, i, :], bank[:].rearrange("p s w -> p (s w)"), ACT.Tanh, bias=c_sb[:, i : i + 1])
+
+        def make_y_all(m0, w):
+            result = ring.tile([P, N // P, w], F32, name="result4", align_bytes=64, bufs=2)
+            for i in range(N // P):
+                make_y(i, m0, w, 1, result)
+            nc.sync.dma_start(out[:, m0 : m0 + w].rearrange("(i p) m -> p i m", p=P), result[:])
+
+        gather_scales()
+        gather_tab(0)
+        turn_scales()
+        gather_tab(1)
+        group_x("S", 0, 0, 256)
+        group_x("S", 1, 0, 256)
+        quantize_x(0, 0, 256)
+        quantize_x(1, 0, 256)
+        make_h(0, 0, 256, "V")
+        group_x("S", 0, 256, 256)
+        make_h(1, 0, 256, "V")
+        group_x("S", 1, 256, 256)
+        gain_h(0, 0)
+        quantize_x(0, 256, 256)
+        quantize_h(0, 0)
+        gain_h(1, 0)
+        quantize_x(1, 256, 256)
+        gather_wd(0, 0)
+        quantize_h(1, 0)
+        gather_wd(0, 1)
+        turn_wd(0)
+        make_h(0, 256, 256, "V")
+        make_h(1, 256, 256, "V")
+        gain_h(0, 256)
+        quantize_wd(0)
+        gather_wd(1, 0)
+        quantize_h(0, 256)
+        gain_h(1, 256)
+        gather_wd(1, 1)
+        quantize_h(1, 256)
+        turn_wd(1)
+        group_x("S", 0, 512, 256)
+        group_x("S", 0, 768, 256)
+        group_x("S", 1, 512, 256)
+        group_x("S", 1, 768, 256)
+        quantize_wd(1)
+        make_y(0, 0, 512, 1)
+        quantize_x(0, 512, 512)
+        gather_wd(2, 0)
+        gather_wd(2, 1)
+        turn_wd(2)
+        quantize_x(1, 512, 512)
+        make_y(1, 0, 512, 1)
+        gather_wd(3, 0)
+        quantize_wd(2)
+        make_h(0, 512, 256, "V")
+        gather_wd(3, 1)
+        turn_wd(3)
+        make_y(2, 0, 512, 1)
+        make_h(1, 512, 256, "V")
+        gain_h(0, 512)
+        quantize_wd(3)
+        make_h(0, 768, 256, "V")
+        quantize_h(0, 512)
+        make_y(3, 0, 512, 1)
+        gain_h(1, 512)
+        make_h(1, 768, 128, "V")
+        quantize_h(1, 512)
+        gain_h(0, 768)
+        make_h(1, 896, 128, "V")
+        quantize_h(0, 768)
+        for i in range(4):
+            make_y(i, 512, 128, 2)
+        gain_h(1, 768)
+        gain_h(1, 896)
+        quantize_h(1, 768)
+        quantize_h(1, 896)
+        make_y_all(768, 128)
+        make_y_all(896, 128)

@@ -38,7 +38,7 @@ def tile_list_sparse_reservoir_control_kernel(tc, x, tab_words, tab_scales, offs
         tab_plane = keep.tile([P, T // 4], I32, name="tab_plane", align_bytes=64)
         nc.vector.memset(tab_plane[:], 0)
         wf_plane = keep.tile([P, 2, N // 4], I32, name="wf_plane", align_bytes=64)
-        nc.vector.memset(wf_plane[:], 0)
+        nc.gpsimd.memset(wf_plane[:], 0)
         warm = keep.tile([P, 8], F32, name="warm")
         nc.vector.memset(warm[:], 0.0)
         for q in range(4):
@@ -47,47 +47,58 @@ def tile_list_sparse_reservoir_control_kernel(tc, x, tab_words, tab_scales, offs
         nc.scalar.activation(warm_out[:], warm[:], ACT.Tanh)
 
         tab = [keep.tile([P, T], I32, name=f"tab{a}", align_bytes=64) for a in range(2)]
-        wd_raw = [keep.tile([P, T], F32, name=f"wd_raw{i}", align_bytes=64) for i in range(N // P)]
+        wd_raw = {}
         wf = keep.tile([P, 2, 2 * N // 4], I32, name="wf", align_bytes=64)
         g_sb = keep.tile([P, 2, PACK], F32, name="g_sb")
         c_sb = keep.tile([P, N // P], F32, name="c_sb")
-        x_raw = keep.tile([P, 2, PACK, M], F32, name="x_raw", align_bytes=64)
-        r_sb = keep.tile([P, 2, PACK, M], F32, name="r_sb", align_bytes=64)
+        x_raw = {"name": "x"}
+        r_sb = {"name": "r"}
 
-        def load_tab(a):
-            nc.sync.dma_start(tab[a][:], tab_words[a].rearrange("p t i -> p (t i)").bitcast(I32))
+        def piece(tiles, a, m0, w):
+            for key in tiles:
+                if key != "name" and key[0] == a and key[1] <= m0 and m0 + w <= key[1] + key[2]:
+                    return tiles[key][:, :, m0 - key[1] : m0 - key[1] + w]
+            raise AssertionError("no piece")
 
-        def load_rows(dst, src, a, m0, w):
+        def load_tab(a, queue=nc.sync):
+            queue.dma_start(tab[a][:], tab_words[a].rearrange("p t i -> p (t i)").bitcast(I32))
+
+        def load_rows(dst, src, a, m0, w, queue=nc.sync):
             rows = src[a * PASS : (a + 1) * PASS, m0 : m0 + w]
-            nc.sync.dma_start(dst[:, a, :, m0 : m0 + w], rows.rearrange("(p t) m -> p t m", t=PACK))
+            dst[(a, m0, w)] = keep.tile([P, PACK, w], F32, name=f"{dst['name']}_{a}_{m0}", align_bytes=64)
+            queue.dma_start(dst[(a, m0, w)][:], rows.rearrange("(p t) m -> p t m", t=PACK))
 
-        def load_wd(i):
-            nc.sync.dma_start(wd_raw[i][:], wdT[i * P : (i + 1) * P, :])
+        def load_wd(i, queue=nc.sync):
+            wd_raw[i] = ring.tile([P, T], F32, name="wd_raw", align_bytes=64, bufs=4)
+            queue.dma_start(wd_raw[i][:], wdT[i * P : (i + 1) * P, :])
+
+        def load_wf():
+            nc.sync.dma_start(wf[:], wf_words.bitcast(I32).rearrange("a p e -> p a e"))
 
         def load_small():
-            nc.sync.dma_start(wf[:], wf_words.bitcast(I32).rearrange("a p e -> p a e"))
             for row in range(4):
-                nc.sync.dma_start(wf_plane[row:P:32, :, :], wf_scales.bitcast(I32)[:, row:16:4, :].rearrange("a q e -> q a e"))
+                nc.gpsimd.dma_start(wf_plane[row:P:32, :, :], wf_scales.bitcast(I32)[:, row:16:4, :].rearrange("a q e -> q a e"))
             with nc.allow_non_contiguous_dma(reason="one bias a partition"):
-                nc.sync.dma_start(c_sb[:], c.rearrange("(i p) -> p i", p=P))
+                nc.gpsimd.dma_start(c_sb[:], c.rearrange("(i p) -> p i", p=P))
 
         def load_g():
-            nc.sync.dma_start(g_sb[:], g.rearrange("(b p t) -> p b t", b=2, t=PACK))
+            nc.gpsimd.dma_start(g_sb[:], g.rearrange("(b p t) -> p b t", b=2, t=PACK))
 
-        load_tab(0)
+        load_g()
+        load_small()
+        load_rows(x_raw, x, 1, 0, 256)
         load_tab(1)
         load_rows(x_raw, x, 0, 0, 256)
-        load_rows(x_raw, x, 1, 0, 256)
-        load_g()
-        load_rows(r_sb, r, 0, 0, 256)
-        load_rows(r_sb, r, 1, 0, 256)
+        load_tab(0)
         load_rows(x_raw, x, 0, 256, 256)
         load_rows(x_raw, x, 1, 256, 256)
-        load_wd(0)
+        load_rows(r_sb, r, 0, 0, 256)
+        load_rows(r_sb, r, 1, 0, 256)
         load_rows(r_sb, r, 0, 256, 256)
         load_rows(r_sb, r, 1, 256, 256)
+        load_wf()
+        load_wd(0)
         load_wd(1)
-        load_small()
         load_rows(x_raw, x, 0, 512, 512)
         load_rows(x_raw, x, 1, 512, 512)
         load_wd(2)
@@ -128,7 +139,7 @@ def tile_list_sparse_reservoir_control_kernel(tc, x, tab_words, tab_scales, offs
 
         def group_x(engine, a, m0, w):
             dst = x_grouped[:, a, m0 : m0 + w, :].rearrange("p (c i) t -> p c t i", i=4)
-            src = x_raw[:, a, :, m0 : m0 + w].rearrange("p t (c i) -> p c t i", i=4)
+            src = piece(x_raw, a, m0, w).rearrange("p t (c i) -> p c t i", i=4)
             if engine == "S":
                 nc.scalar.copy(dst, src)
             elif engine == "G":
@@ -162,7 +173,7 @@ def tile_list_sparse_reservoir_control_kernel(tc, x, tab_words, tab_scales, offs
                             start=(a == 0),
                             stop=(a == 1),
                         )
-                nc.vector.tensor_tensor(z[:, t0 : t0 + per_bank, :], bank[:], r_sb[:, b, t0 : t0 + per_bank, cols], ALU.add)
+                nc.vector.tensor_tensor(z[:, t0 : t0 + per_bank, :], bank[:], piece(r_sb, b, m0, w)[:, t0 : t0 + per_bank, :], ALU.add)
             hb = ring.tile([P, w, PACK], BF16, name="hb", align_bytes=64, bufs=3)
             if mode == "S":
                 th = ring.tile([P, PACK, w], F32, name="th", align_bytes=64)
@@ -257,72 +268,74 @@ def tile_list_sparse_reservoir_control_kernel(tc, x, tab_words, tab_scales, offs
                 make_y(i, m0, w, 1, result)
             nc.sync.dma_start(out[:, m0 : m0 + w].rearrange("(i p) m -> p i m", p=P), result[:])
 
-        gather_scales()
-        gather_tab(0)
-        turn_scales()
-        gather_tab(1)
-        group_x("S", 0, 0, 256)
-        group_x("S", 1, 0, 256)
-        quantize_x(0, 0, 256)
-        quantize_x(1, 0, 256)
-        make_h(0, 0, 256, "V")
         group_x("S", 0, 256, 256)
-        make_h(1, 0, 256, "V")
         group_x("S", 1, 256, 256)
-        gain_h(0, 0)
-        quantize_x(0, 256, 256)
-        quantize_h(0, 0)
-        gain_h(1, 0)
-        quantize_x(1, 256, 256)
-        gather_wd(0, 0)
-        quantize_h(1, 0)
-        gather_wd(0, 1)
-        turn_wd(0)
-        make_h(0, 256, 256, "V")
-        make_h(1, 256, 256, "V")
-        gain_h(0, 256)
-        quantize_wd(0)
-        gather_wd(1, 0)
-        quantize_h(0, 256)
-        gain_h(1, 256)
-        gather_wd(1, 1)
-        quantize_h(1, 256)
-        turn_wd(1)
-        group_x("S", 0, 512, 256)
-        group_x("S", 0, 768, 256)
+        group_x("V", 1, 0, 256)
+        gather_scales()
+        group_x("S", 0, 0, 256)
+        gather_tab(0)
+        quantize_x(0, 0, 256)
         group_x("S", 1, 512, 256)
+        turn_scales()
+        gather_wd(3, 1)
+        gather_tab(1)
+        quantize_x(1, 0, 256)
+        group_x("S", 0, 768, 256)
+        make_h(0, 0, 256, "S")
+        gather_wd(0, 0)
+        gain_h(0, 0)
+        quantize_h(0, 0)
+        gather_wd(0, 1)
+        quantize_x(1, 256, 256)
+        quantize_x(0, 256, 256)
+        make_h(1, 0, 256, "S")
+        make_h(0, 256, 256, "S")
+        gain_h(1, 0)
+        gather_wd(2, 0)
+        gain_h(0, 256)
+        quantize_h(1, 0)
+        turn_wd(0)
+        gather_wd(1, 1)
+        gather_wd(3, 0)
+        group_x("S", 0, 512, 256)
+        make_h(1, 256, 256, "S")
+        gain_h(1, 256)
+        gather_wd(1, 0)
+        turn_wd(3)
+        quantize_h(0, 256)
+        gather_wd(2, 1)
+        quantize_wd(0)
+        turn_wd(1)
+        turn_wd(2)
+        quantize_h(1, 256)
+        quantize_wd(3)
+        quantize_x(0, 512, 512)
         group_x("S", 1, 768, 256)
         quantize_wd(1)
-        make_y(0, 0, 512, 1)
-        quantize_x(0, 512, 512)
-        gather_wd(2, 0)
-        gather_wd(2, 1)
-        turn_wd(2)
+        quantize_wd(2)
+        make_y(2, 0, 512, 1)
         quantize_x(1, 512, 512)
         make_y(1, 0, 512, 1)
-        gather_wd(3, 0)
-        quantize_wd(2)
         make_h(0, 512, 256, "V")
-        gather_wd(3, 1)
-        turn_wd(3)
-        make_y(2, 0, 512, 1)
-        make_h(1, 512, 256, "V")
-        gain_h(0, 512)
-        quantize_wd(3)
-        make_h(0, 768, 256, "V")
-        quantize_h(0, 512)
         make_y(3, 0, 512, 1)
+        make_h(1, 512, 256, "S")
+        gain_h(0, 512)
+        quantize_h(0, 512)
+        make_h(0, 768, 256, "V")
+        make_y(0, 0, 512, 1)
         gain_h(1, 512)
-        make_h(1, 768, 128, "V")
         quantize_h(1, 512)
+        make_y(3, 512, 128, 2)
+        make_h(1, 768, 128, "S")
+        make_y(0, 512, 128, 2)
+        make_y(1, 512, 128, 2)
         gain_h(0, 768)
-        make_h(1, 896, 128, "V")
         quantize_h(0, 768)
-        for i in range(4):
-            make_y(i, 512, 128, 2)
         gain_h(1, 768)
+        make_h(1, 896, 128, "V")
+        make_y(2, 512, 128, 2)
         gain_h(1, 896)
-        quantize_h(1, 768)
         quantize_h(1, 896)
-        make_y_all(768, 128)
         make_y_all(896, 128)
+        quantize_h(1, 768)
+        make_y_all(768, 128)

@@ -28,9 +28,17 @@ def tile_list_sparse_reservoir_control_kernel(tc, x, tab_words, tab_scales, offs
     nc = tc.nc
     with ExitStack() as ctx:
         keep = ctx.enter_context(tc.tile_pool(name="keep", bufs=1))
-        ring = ctx.enter_context(tc.tile_pool(name="ring", bufs=3))
-        psum_p = ctx.enter_context(tc.psum_pool(name="psum_p", bufs=3))
-        psum_y = ctx.enter_context(tc.psum_pool(name="psum_y", bufs=5))
+        ring = ctx.enter_context(tc.tile_pool(name="ring", bufs=1))
+        psum = ctx.enter_context(tc.psum_pool(name="psum", bufs=8))
+
+        def vector_tile(shape, dtype):
+            return ring.tile(shape, dtype, name="vector_out", align_bytes=64, bufs=52)
+
+        def scalar_tile(shape, dtype):
+            return ring.tile(shape, dtype, name="scalar_out", align_bytes=64, bufs=10)
+
+        def bank_tile(shape):
+            return psum.tile(shape, F32, name="bank")
 
         offsets = keep.tile([P, S // 16], U16, name="offsets")
         nc.sync.dma_start(offsets[:], offs)
@@ -45,73 +53,44 @@ def tile_list_sparse_reservoir_control_kernel(tc, x, tab_words, tab_scales, offs
             nc.sync.dma_start(tab_plane[32 * q : 32 * q + 8, :], tab_scales[:, 4 * q : 4 * q + 4, :].bitcast(I32))
         warm_out = keep.tile([P, 8], F32, name="warm_out")
         nc.scalar.activation(warm_out[:], warm[:], ACT.Tanh)
-
-        tab = [keep.tile([P, T], I32, name=f"tab{a}", align_bytes=64) for a in range(2)]
-        wd_raw = {}
-        wf = keep.tile([P, 2, 2 * N // 4], I32, name="wf", align_bytes=64)
-        g_sb = keep.tile([P, 2, PACK], F32, name="g_sb")
-        c_sb = keep.tile([P, N // P], F32, name="c_sb")
-        x_raw = {"name": "x"}
-        r_sb = {"name": "r"}
-
-        def piece(tiles, a, m0, w):
-            for key in tiles:
-                if key != "name" and key[0] == a and key[1] <= m0 and m0 + w <= key[1] + key[2]:
-                    return tiles[key][:, :, m0 - key[1] : m0 - key[1] + w]
-            raise AssertionError("no piece")
-
-        def load_tab(a, queue=nc.sync):
-            queue.dma_start(tab[a][:], tab_words[a].rearrange("p t i -> p (t i)").bitcast(I32))
-
-        def load_rows(dst, src, a, m0, w, queue=nc.sync):
-            rows = src[a * PASS : (a + 1) * PASS, m0 : m0 + w]
-            dst[(a, m0, w)] = keep.tile([P, PACK, w], F32, name=f"{dst['name']}_{a}_{m0}", align_bytes=64)
-            queue.dma_start(dst[(a, m0, w)][:], rows.rearrange("(p t) m -> p t m", t=PACK))
-
-        def load_wd(i, queue=nc.sync):
-            wd_raw[i] = ring.tile([P, T], F32, name="wd_raw", align_bytes=64, bufs=4)
-            queue.dma_start(wd_raw[i][:], wdT[i * P : (i + 1) * P, :])
-
-        def load_wf():
-            nc.sync.dma_start(wf[:], wf_words.bitcast(I32).rearrange("a p e -> p a e"))
-
-        def load_small():
-            for row in range(4):
-                nc.gpsimd.dma_start(wf_plane[row:P:32, :, :], wf_scales.bitcast(I32)[:, row:16:4, :].rearrange("a q e -> q a e"))
-            with nc.allow_non_contiguous_dma(reason="one bias a partition"):
-                nc.gpsimd.dma_start(c_sb[:], c.rearrange("(i p) -> p i", p=P))
-
-        def load_g():
-            nc.gpsimd.dma_start(g_sb[:], g.rearrange("(b p t) -> p b t", b=2, t=PACK))
-
-        load_g()
-        load_small()
-        load_rows(x_raw, x, 1, 0, 256)
-        load_tab(1)
-        load_rows(x_raw, x, 0, 0, 256)
-        load_tab(0)
-        load_rows(x_raw, x, 0, 256, 256)
-        load_rows(x_raw, x, 1, 256, 256)
-        load_rows(r_sb, r, 0, 0, 256)
-        load_rows(r_sb, r, 1, 0, 256)
-        load_rows(r_sb, r, 0, 256, 256)
-        load_rows(r_sb, r, 1, 256, 256)
-        load_wf()
-        load_wd(0)
-        load_wd(1)
-        load_rows(x_raw, x, 0, 512, 512)
-        load_rows(x_raw, x, 1, 512, 512)
-        load_wd(2)
-        load_wd(3)
-        load_rows(r_sb, r, 0, 512, 512)
-        load_rows(r_sb, r, 1, 512, 512)
-
         ident = keep.tile([P, P], F32, name="ident", align_bytes=64)
         make_identity(nc, ident[:])
 
+        wf = keep.tile([P, 2, 2 * N // 4], I32, name="wf", align_bytes=64)
+        g_sb = keep.tile([P, 2, PACK], F32, name="g_sb")
+        c_sb = keep.tile([P, N // P], F32, name="c_sb")
         v_codes = [keep.tile([P, S], U32, name=f"v_codes{a}", align_bytes=64) for a in range(2)]
         v_plane_list = keep.tile([P, S], U8, name="v_plane_list", align_bytes=64)
         v_plane = keep.tile([P, S], U8, name="v_plane", align_bytes=64)
+        tab, wd_raw, x_raw, r_sb = {}, {}, {}, {}
+        x_grouped, x_mx, h_mx, wd_mx = {}, {}, {}, {}
+        staged, gained, picked, wd_grouped = {}, {}, {}, {}
+
+        def load_tab(a, queue=nc.sync):
+            tab[a] = ring.tile([P, T], I32, name="table", align_bytes=64, bufs=3)
+            queue.dma_start(tab[a][:], tab_words[a].rearrange("p t i -> p (t i)").bitcast(I32))
+
+        def load_wd(i, queue=nc.sync):
+            wd_raw[i] = ring.tile([P, T], F32, name="table", align_bytes=64, bufs=3)
+            queue.dma_start(wd_raw[i][:], wdT[i * P : (i + 1) * P, :])
+
+        def load_rows(dst, src, a, m0, w, queue=nc.sync):
+            rows = src[a * PASS : (a + 1) * PASS, m0 : m0 + w]
+            dst[(a, m0)] = ring.tile([P, PACK, w], F32, name="rows", align_bytes=64, bufs=10)
+            queue.dma_start(dst[(a, m0)][:], rows.rearrange("(p t) m -> p t m", t=PACK))
+
+        def load_wf(queue=nc.sync):
+            queue.dma_start(wf[:], wf_words.bitcast(I32).rearrange("a p e -> p a e"))
+
+        def load_wfs(row, queue=nc.sync):
+            queue.dma_start(wf_plane[row:P:32, :, :], wf_scales.bitcast(I32)[:, row:16:4, :].rearrange("a q e -> q a e"))
+
+        def load_c(unused, queue=nc.sync):
+            with nc.allow_non_contiguous_dma(reason="one bias a partition"):
+                queue.dma_start(c_sb[:], c.rearrange("(i p) -> p i", p=P))
+
+        def load_g(unused, queue=nc.sync):
+            queue.dma_start(g_sb[:], g.rearrange("(b p t) -> p b t", b=2, t=PACK))
 
         def gather_tab(a):
             nc.vector.tensor_copy(
@@ -128,214 +107,295 @@ def tile_list_sparse_reservoir_control_kernel(tc, x, tab_words, tab_scales, offs
                 v_plane_list[:].rearrange("k (b p t) -> k b p t", b=2, t=PACK),
             )
 
-        x_codes = keep.tile([P, 2, M], U32, name="x_codes", align_bytes=64)
-        x_plane = keep.tile([P, 2, M], U8, name="x_plane", align_bytes=64)
-        h_codes = keep.tile([P, 2, M], U32, name="h_codes", align_bytes=64)
-        h_plane = keep.tile([P, 2, M], U8, name="h_plane", align_bytes=64)
-        wd_codes = keep.tile([P, N // P, 2 * P], U32, name="wd_codes", align_bytes=64)
-        wd_plane = keep.tile([P, N // P, 2 * P], U8, name="wd_plane", align_bytes=64)
-        x_grouped = keep.tile([P, 2, M, PACK], BF16, name="x_grouped", align_bytes=64)
-        staged = {}
+        def quantize(values, width):
+            mx = vector_tile([P, 5 * width], U8)
+            nc.vector.quantize_mx(out=mx[:, 0 : 4 * width].bitcast(FP8X4), scales=mx[:, 4 * width : 5 * width], in_=values)
+            return mx, width
+
+        def operand(mx_width, start):
+            mx, width = mx_width
+            return mx[:, 4 * start : 4 * (start + P)].bitcast(FP8X4), mx[:, 4 * width + start : 4 * width + start + P]
+
+        def columns(tiles, a, m0):
+            start = max(key[1] for key in tiles if key[0] == a and key[1] <= m0)
+            return operand(tiles[(a, start)], m0 - start)
 
         def group_x(engine, a, m0, w):
-            dst = x_grouped[:, a, m0 : m0 + w, :].rearrange("p (c i) t -> p c t i", i=4)
-            src = piece(x_raw, a, m0, w).rearrange("p t (c i) -> p c t i", i=4)
+            src = x_raw[(a, m0)][:].rearrange("p t (c i) -> p c t i", i=4)
             if engine == "S":
-                nc.scalar.copy(dst, src)
-            elif engine == "G":
-                nc.gpsimd.tensor_copy(dst, src)
+                x_grouped[(a, m0)] = scalar_tile([P, w, PACK], BF16)
+                nc.scalar.copy(x_grouped[(a, m0)][:].rearrange("p (c i) t -> p c t i", i=4), src)
             else:
-                nc.vector.tensor_copy(dst, src)
+                x_grouped[(a, m0)] = vector_tile([P, w, PACK], BF16)
+                nc.vector.tensor_copy(x_grouped[(a, m0)][:].rearrange("p (c i) t -> p c t i", i=4), src)
 
         def quantize_x(a, m0, w):
-            cols = slice(m0, m0 + w)
-            nc.vector.quantize_mx(
-                out=x_codes[:, a, cols].bitcast(FP8X4),
-                scales=x_plane[:, a, cols],
-                in_=x_grouped[:, a, cols, :].rearrange("p m t -> p (m t)"),
-            )
+            x_mx[(a, m0)] = quantize(x_grouped[(a, m0)][:].rearrange("p m t -> p (m t)"), w)
+
+        summed = {}
+
+        def add_h(b, m1):
+            bank = bank_tile([P, PACK, P])
+            for t in range(PACK):
+                jcols = slice(b * PASS + t * P, b * PASS + (t + 1) * P)
+                for a in range(2):
+                    codes, plane = columns(x_mx, a, m1)
+                    nc.tensor.matmul_mx(
+                        out=bank[:, t, :],
+                        lhsT=v_codes[a][:, jcols].bitcast(FP8X4),
+                        lhsT_scale=v_plane[4 * a : P, jcols],
+                        rhs=codes,
+                        rhs_scale=plane,
+                        start=(a == 0),
+                        stop=(a == 1),
+                    )
+            z = vector_tile([P, PACK, P], F32)
+            start = m1 // 256 * 256
+            nc.vector.tensor_tensor(z[:], bank[:], r_sb[(b, start)][:, :, m1 - start : m1 - start + P], ALU.add)
+            summed[(b, m1)] = z
 
         def make_h(b, m0, w, mode):
-            cols = slice(m0, m0 + w)
-            per_bank = BANK // w
-            z = ring.tile([P, PACK, w], F32, name="z", align_bytes=64)
-            for t0 in range(0, PACK, per_bank):
-                bank = psum_p.tile([P, per_bank, w], F32, name="p_bank")
-                for t in range(t0, t0 + per_bank):
-                    jcols = slice(b * PASS + t * P, b * PASS + (t + 1) * P)
-                    for a in range(2):
-                        nc.tensor.matmul_mx(
-                            out=bank[:, t - t0, :],
-                            lhsT=v_codes[a][:, jcols].bitcast(FP8X4),
-                            lhsT_scale=v_plane[4 * a : P, jcols],
-                            rhs=x_codes[:, a, cols].bitcast(FP8X4),
-                            rhs_scale=x_plane[:, a, cols],
-                            start=(a == 0),
-                            stop=(a == 1),
-                        )
-                nc.vector.tensor_tensor(z[:, t0 : t0 + per_bank, :], bank[:], piece(r_sb, b, m0, w)[:, t0 : t0 + per_bank, :], ALU.add)
-            hb = ring.tile([P, w, PACK], BF16, name="hb", align_bytes=64, bufs=3)
+            th = scalar_tile([P, w // P, PACK * P], F32)
+            for m1 in range(m0, m0 + w, P):
+                z = summed[(b, m1)]
+                part = th[:, (m1 - m0) // P, :]
+                if mode == "S":
+                    nc.scalar.activation(part, z[:].rearrange("p t m -> p (t m)"), ACT.Tanh)
+                else:
+                    nc.scalar.activation(
+                        part.rearrange("p (c i t) -> p c t i", i=4, t=PACK),
+                        z[:].rearrange("p t (c i) -> p c t i", i=4),
+                        ACT.Tanh,
+                    )
+            staged[(b, m0)] = (th, mode, w)
+
+        def scale_h(b, m0):
+            th, mode, w = staged[(b, m0)]
             if mode == "S":
-                th = ring.tile([P, PACK, w], F32, name="th", align_bytes=64)
-                nc.scalar.activation(th[:], z[:], ACT.Tanh)
-                slots = ring.tile([P, PACK, w], BF16, name="slots", align_bytes=64)
+                slots = scalar_tile([P, PACK, w], BF16)
                 for t in range(PACK):
-                    nc.scalar.activation(slots[:, t, :], th[:, t, :], ACT.Copy, scale=g_sb[:, b, t : t + 1])
-                staged[(b, m0)] = (slots, hb, mode, w)
-            else:
-                th = ring.tile([P, w, PACK], F32, name="th", align_bytes=64)
-                nc.scalar.activation(
-                    th[:].rearrange("p (c i) t -> p c t i", i=4),
-                    z[:].rearrange("p t (c i) -> p c t i", i=4),
-                    ACT.Tanh,
-                )
-                staged[(b, m0)] = (th, hb, mode, w)
+                    nc.scalar.activation(
+                        slots[:, t, :].rearrange("p (s m) -> p s m", m=P),
+                        th[:, :, t * P : (t + 1) * P],
+                        ACT.Copy,
+                        scale=g_sb[:, b, t : t + 1],
+                    )
+                staged[(b, m0)] = (slots, mode, w)
 
         def gain_h(b, m0):
-            th, hb, mode, w = staged[(b, m0)]
+            th, mode, w = staged[(b, m0)]
+            hb = vector_tile([P, w, PACK], BF16)
             if mode == "S":
                 nc.vector.tensor_copy(hb[:].rearrange("p (c i) t -> p c t i", i=4), th[:].rearrange("p t (c i) -> p c t i", i=4))
-            elif mode == "G":
-                nc.gpsimd.tensor_tensor(hb[:], th[:], g_sb[:, b : b + 1, :].to_broadcast([P, w, PACK]), ALU.mult)
             else:
-                nc.vector.tensor_tensor(hb[:], th[:], g_sb[:, b : b + 1, :].to_broadcast([P, w, PACK]), ALU.mult)
+                nc.vector.tensor_tensor(
+                    hb[:],
+                    th[:].rearrange("p s (m t) -> p (s m) t", t=PACK),
+                    g_sb[:, b : b + 1, :].to_broadcast([P, w, PACK]),
+                    ALU.mult,
+                )
+            gained[(b, m0)] = (hb, w)
 
         def quantize_h(b, m0):
-            th, hb, mode, w = staged[(b, m0)]
-            cols = slice(m0, m0 + w)
-            nc.vector.quantize_mx(
-                out=h_codes[:, b, cols].bitcast(FP8X4),
-                scales=h_plane[:, b, cols],
-                in_=hb[:].rearrange("p m t -> p (m t)"),
-            )
-
-        picked = [keep.tile([P, S], BF16, name=f"wd_picked{i}", align_bytes=64) for i in range(N // P)]
-        wd_grouped = [keep.tile([P, S], BF16, name=f"wd_grouped{i}", align_bytes=64) for i in range(N // P)]
+            hb, w = gained[(b, m0)]
+            h_mx[(b, m0)] = quantize(hb[:].rearrange("p m t -> p (m t)"), w)
 
         def gather_wd(i, b):
+            picked[(i, b)] = vector_tile([P, PASS], BF16)
             nc.vector.tensor_copy(
-                picked[i][:, b * PASS : (b + 1) * PASS].rearrange("n (u p e) -> n p u e", u=2, e=2),
+                picked[(i, b)][:].rearrange("n (u p e) -> n p u e", u=2, e=2),
                 wd_raw[i][:].indirect(offsets[:, 32 * b : 32 * (b + 1)]),
             )
 
         def turn_wd(i):
-            words = picked[i][:].bitcast(F32)
-            turned = psum_y.tile([P, 4, P], F32, name="y_bank")
-            for s in range(4):
-                nc.tensor.transpose(turned[:, s, :], words[:, s * P : (s + 1) * P], ident[:])
+            turned = bank_tile([P, 4, P])
+            for b in range(2):
+                words = picked[(i, b)][:].bitcast(F32)
+                for u in range(2):
+                    nc.tensor.transpose(turned[:, 2 * b + u, :], words[:, u * P : (u + 1) * P], ident[:])
+            wd_grouped[i] = scalar_tile([P, S], BF16)
             nc.scalar.copy(
                 wd_grouped[i][:].bitcast(F32).rearrange("p (b n u) -> p b n u", b=2, u=2),
                 turned[:].rearrange("p (b u) n -> p b n u", b=2),
             )
 
         def quantize_wd(i):
-            nc.vector.quantize_mx(out=wd_codes[:, i, :].bitcast(FP8X4), scales=wd_plane[:, i, :], in_=wd_grouped[i][:])
+            wd_mx[i] = quantize(wd_grouped[i][:], 2 * P)
 
-        def make_y(i, m0, w, groups, result=None):
-            bank = psum_y.tile([P, groups, w], F32, name="y_bank")
+        opened = {}
+
+        def open_y(i, m0):
+            make_y(i, m0, P, 1, True)
+
+        def make_y(i, m0, w, groups, only_open=False):
+            fresh = (i, m0) not in opened
+            if fresh:
+                opened[(i, m0)] = bank_tile([P, groups, P])
+            bank = opened[(i, m0)]
             for s in range(groups):
-                cols = slice(m0 + s * w, m0 + (s + 1) * w)
-                for a in range(2):
+                for a in range(2 if fresh else 0):
+                    codes, plane = columns(x_mx, a, m0 + s * P)
                     nc.tensor.matmul_mx(
                         out=bank[:, s, :],
                         lhsT=wf[:, a, :].bitcast(U8)[:, 2 * i * P : 2 * (i + 1) * P].bitcast(FP4X4),
                         lhsT_scale=wf_plane[:, a, :].bitcast(U8)[:, i * P : (i + 1) * P],
-                        rhs=x_codes[:, a, cols].bitcast(FP8X4),
-                        rhs_scale=x_plane[:, a, cols],
+                        rhs=codes,
+                        rhs_scale=plane,
                         start=(a == 0),
                         stop=False,
                     )
+                if only_open:
+                    return
                 for b in range(2):
+                    codes, plane = columns(h_mx, b, m0 + s * P)
+                    weights, weight_plane = operand(wd_mx[i], b * P)
                     nc.tensor.matmul_mx(
                         out=bank[:, s, :],
-                        lhsT=wd_codes[:, i, b * P : (b + 1) * P].bitcast(FP8X4),
-                        lhsT_scale=wd_plane[:, i, b * P : (b + 1) * P],
-                        rhs=h_codes[:, b, cols].bitcast(FP8X4),
-                        rhs_scale=h_plane[:, b, cols],
+                        lhsT=weights,
+                        lhsT_scale=weight_plane,
+                        rhs=codes,
+                        rhs_scale=plane,
                         start=False,
                         stop=(b == 1),
                     )
-            if result is None:
-                result = ring.tile([P, groups * w], F32, name="result", align_bytes=64, bufs=4)
-                nc.scalar.activation(result[:], bank[:].rearrange("p s w -> p (s w)"), ACT.Tanh, bias=c_sb[:, i : i + 1])
-                nc.sync.dma_start(out[i * P : (i + 1) * P, m0 : m0 + groups * w], result[:])
-            else:
-                nc.scalar.activation(result[:, i, :], bank[:].rearrange("p s w -> p (s w)"), ACT.Tanh, bias=c_sb[:, i : i + 1])
+            result = scalar_tile([P, groups * P], F32)
+            nc.scalar.activation(result[:], bank[:].rearrange("p s w -> p (s w)"), ACT.Tanh, bias=c_sb[:, i : i + 1])
+            nc.sync.dma_start(out[i * P : (i + 1) * P, m0 : m0 + groups * P], result[:])
 
-        def make_y_all(m0, w):
-            result = ring.tile([P, N // P, w], F32, name="result4", align_bytes=64, bufs=2)
-            for i in range(N // P):
-                make_y(i, m0, w, 1, result)
-            nc.sync.dma_start(out[:, m0 : m0 + w].rearrange("(i p) m -> p i m", p=P), result[:])
-
-        group_x("S", 0, 256, 256)
-        group_x("S", 1, 256, 256)
-        group_x("V", 1, 0, 256)
-        gather_scales()
+        load_tab(1, nc.scalar)
+        load_rows(x_raw, x, 0, 0, 256)
+        load_rows(x_raw, x, 1, 256, 256, nc.scalar)
+        load_rows(x_raw, x, 1, 0, 256, nc.scalar)
+        load_rows(x_raw, x, 0, 256, 256)
+        load_rows(r_sb, r, 0, 0, 256)
+        load_g(0, nc.scalar)
         group_x("S", 0, 0, 256)
+        gather_scales()
+        load_tab(0)
+        load_rows(r_sb, r, 1, 0, 256)
+        group_x("S", 1, 256, 256)
+        group_x("S", 1, 0, 256)
+        load_wfs(2)
         gather_tab(0)
+        load_wd(0)
+        group_x("S", 0, 256, 256)
+        load_rows(r_sb, r, 0, 256, 256)
+        load_rows(x_raw, x, 0, 512, 256)
         quantize_x(0, 0, 256)
-        group_x("S", 1, 512, 256)
-        turn_scales()
-        gather_wd(3, 1)
-        gather_tab(1)
         quantize_x(1, 0, 256)
-        group_x("S", 0, 768, 256)
-        make_h(0, 0, 256, "S")
-        gather_wd(0, 0)
-        gain_h(0, 0)
-        quantize_h(0, 0)
-        gather_wd(0, 1)
         quantize_x(1, 256, 256)
-        quantize_x(0, 256, 256)
+        turn_scales()
+        gather_tab(1)
+        add_h(0, 128)
+        add_h(0, 0)
+        add_h(1, 0)
+        add_h(1, 128)
+        make_h(0, 0, 256, "S")
         make_h(1, 0, 256, "S")
-        make_h(0, 256, 256, "S")
+        scale_h(1, 0)
+        quantize_x(0, 256, 256)
+        load_rows(x_raw, x, 1, 512, 256)
+        load_rows(r_sb, r, 1, 256, 256)
+        scale_h(0, 0)
+        gather_wd(0, 1)
+        gather_wd(0, 0)
         gain_h(1, 0)
+        add_h(0, 256)
+        group_x("S", 0, 512, 256)
+        quantize_h(1, 0)
+        gain_h(0, 0)
+        add_h(1, 384)
+        group_x("S", 1, 512, 256)
+        load_wd(1)
+        load_wfs(3)
+        add_h(0, 384)
+        quantize_x(1, 512, 256)
+        make_h(0, 256, 256, "S")
+        quantize_x(0, 512, 256)
+        add_h(1, 256)
+        gather_wd(1, 0)
+        gather_wd(1, 1)
+        load_wd(2)
+        load_rows(x_raw, x, 1, 768, 256)
+        load_wfs(1)
+        load_wf()
+        turn_wd(0)
+        scale_h(0, 256)
+        make_h(1, 256, 256, "S")
+        quantize_wd(0)
+        load_rows(r_sb, r, 0, 512, 256)
+        gather_wd(2, 1)
+        load_wfs(0)
+        load_rows(x_raw, x, 0, 768, 256)
+        load_rows(r_sb, r, 1, 512, 256)
+        quantize_h(0, 0)
+        turn_wd(1)
+        group_x("S", 1, 768, 256)
         gather_wd(2, 0)
         gain_h(0, 256)
-        quantize_h(1, 0)
-        turn_wd(0)
-        gather_wd(1, 1)
-        gather_wd(3, 0)
-        group_x("S", 0, 512, 256)
-        make_h(1, 256, 256, "S")
-        gain_h(1, 256)
-        gather_wd(1, 0)
-        turn_wd(3)
-        quantize_h(0, 256)
-        gather_wd(2, 1)
-        quantize_wd(0)
-        turn_wd(1)
-        turn_wd(2)
-        quantize_h(1, 256)
-        quantize_wd(3)
-        quantize_x(0, 512, 512)
-        group_x("S", 1, 768, 256)
+        scale_h(1, 256)
         quantize_wd(1)
+        load_wd(3)
+        add_h(0, 512)
+        quantize_h(0, 256)
+        load_c(0)
+        add_h(0, 640)
+        turn_wd(2)
+        quantize_x(1, 768, 256)
+        make_h(0, 512, 256, "S")
+        group_x("S", 0, 768, 256)
+        gain_h(1, 256)
+        add_h(1, 512)
+        quantize_h(1, 256)
+        load_rows(r_sb, r, 0, 768, 256)
+        add_h(1, 640)
+        quantize_x(0, 768, 256)
         quantize_wd(2)
-        make_y(2, 0, 512, 1)
-        quantize_x(1, 512, 512)
-        make_y(1, 0, 512, 1)
-        make_h(0, 512, 256, "V")
-        make_y(3, 0, 512, 1)
+        gather_wd(3, 0)
         make_h(1, 512, 256, "S")
+        load_rows(r_sb, r, 1, 768, 256)
+        scale_h(0, 512)
+        make_y(0, 0, 128, 4)
+        make_y(1, 0, 128, 4)
+        gather_wd(3, 1)
+        add_h(0, 768)
+        scale_h(1, 512)
+        add_h(1, 896)
+        add_h(1, 768)
+        add_h(0, 896)
+        turn_wd(3)
+        make_h(1, 768, 128, "V")
+        quantize_wd(3)
+        make_h(0, 768, 128, "V")
         gain_h(0, 512)
-        quantize_h(0, 512)
-        make_h(0, 768, 256, "V")
-        make_y(0, 0, 512, 1)
-        gain_h(1, 512)
-        quantize_h(1, 512)
-        make_y(3, 512, 128, 2)
-        make_h(1, 768, 128, "S")
-        make_y(0, 512, 128, 2)
-        make_y(1, 512, 128, 2)
-        gain_h(0, 768)
-        quantize_h(0, 768)
-        gain_h(1, 768)
+        make_h(0, 896, 128, "S")
+        make_y(2, 0, 128, 4)
+        scale_h(0, 896)
+        scale_h(1, 768)
         make_h(1, 896, 128, "V")
-        make_y(2, 512, 128, 2)
-        gain_h(1, 896)
-        quantize_h(1, 896)
-        make_y_all(896, 128)
+        scale_h(1, 896)
+        scale_h(0, 768)
+        gain_h(1, 512)
+        quantize_h(0, 512)
+        quantize_h(1, 512)
+        gain_h(1, 768)
+        make_y(3, 0, 128, 4)
+        open_y(2, 896)
+        gain_h(0, 768)
         quantize_h(1, 768)
-        make_y_all(768, 128)
+        open_y(1, 896)
+        quantize_h(0, 768)
+        open_y(0, 896)
+        gain_h(1, 896)
+        make_y(2, 512, 128, 3)
+        gain_h(0, 896)
+        make_y(1, 512, 128, 3)
+        quantize_h(1, 896)
+        quantize_h(0, 896)
+        make_y(3, 512, 128, 3)
+        open_y(3, 896)
+        make_y(3, 896, 128, 1)
+        make_y(0, 512, 128, 3)
+        make_y(0, 896, 128, 1)
+        make_y(1, 896, 128, 1)
+        make_y(2, 896, 128, 1)

@@ -32,7 +32,7 @@ def tile_list_sparse_reservoir_control_kernel(tc, x, tab_words, tab_scales, offs
         psum = ctx.enter_context(tc.psum_pool(name="psum", bufs=8))
 
         def vector_tile(shape, dtype):
-            return ring.tile(shape, dtype, name="vector_out", align_bytes=64, bufs=52)
+            return ring.tile(shape, dtype, name="vector_out", align_bytes=64, bufs=50)
 
         def scalar_tile(shape, dtype):
             return ring.tile(shape, dtype, name="scalar_out", align_bytes=64, bufs=10)
@@ -57,6 +57,8 @@ def tile_list_sparse_reservoir_control_kernel(tc, x, tab_words, tab_scales, offs
         make_identity(nc, ident[:])
 
         wf = keep.tile([P, 2, 2 * N // 4], I32, name="wf", align_bytes=64)
+        vectors = keep.tile([P, PASS], F32, name="vectors", align_bytes=64)
+        nc.gpsimd.memset(vectors[:], 0.0)
         g_sb = keep.tile([P, 2, PACK], F32, name="g_sb")
         c_sb = keep.tile([P, N // P], F32, name="c_sb")
         v_codes = [keep.tile([P, S], U32, name=f"v_codes{a}", align_bytes=64) for a in range(2)]
@@ -86,11 +88,22 @@ def tile_list_sparse_reservoir_control_kernel(tc, x, tab_words, tab_scales, offs
             queue.dma_start(wf_plane[row:P:32, :, :], wf_scales.bitcast(I32)[:, row:16:4, :].rearrange("a q e -> q a e"))
 
         def load_c(unused, queue=nc.sync):
-            with nc.allow_non_contiguous_dma(reason="one bias a partition"):
-                queue.dma_start(c_sb[:], c.rearrange("(i p) -> p i", p=P))
+            queue.dma_start(vectors[2:3, :], c.rearrange("(o n) -> o n", o=1))
+
+        def turn_c():
+            turned = bank_tile([P, 4, P])
+            for i in range(N // P):
+                nc.tensor.transpose(turned[:, i, :], vectors[:, i * P : (i + 1) * P], ident[:])
+            nc.scalar.copy(c_sb[:], turned[:, :, 2])
+
+        def turn_g():
+            turned = bank_tile([P, 4, P])
+            for t in range(PACK):
+                nc.tensor.transpose(turned[:, t, :], vectors[:, t:PASS:PACK], ident[:])
+            nc.scalar.copy(g_sb[:], turned[:, :, 0:2].rearrange("p t b -> p b t"))
 
         def load_g(unused, queue=nc.sync):
-            queue.dma_start(g_sb[:], g.rearrange("(b p t) -> p b t", b=2, t=PACK))
+            queue.dma_start(vectors[0:2, :], g.rearrange("(b j) -> b j", b=2))
 
         def gather_tab(a):
             nc.vector.tensor_copy(
@@ -103,8 +116,8 @@ def tile_list_sparse_reservoir_control_kernel(tc, x, tab_words, tab_scales, offs
 
         def turn_scales():
             nc.vector.tensor_copy(
-                v_plane[:].rearrange("k (b t p) -> k b p t", b=2, t=PACK),
-                v_plane_list[:].rearrange("k (b p t) -> k b p t", b=2, t=PACK),
+                v_plane[:].rearrange("k (b t p) -> k b t p", b=2, t=PACK),
+                v_plane_list[:].rearrange("k (b p t) -> k b t p", b=2, t=PACK),
             )
 
         def quantize(values, width):
@@ -200,19 +213,16 @@ def tile_list_sparse_reservoir_control_kernel(tc, x, tab_words, tab_scales, offs
             hb, w = gained[(b, m0)]
             h_mx[(b, m0)] = quantize(hb[:].rearrange("p m t -> p (m t)"), w)
 
-        def gather_wd(i, b):
-            picked[(i, b)] = vector_tile([P, PASS], BF16)
-            nc.vector.tensor_copy(
-                picked[(i, b)][:].rearrange("n (u p e) -> n p u e", u=2, e=2),
-                wd_raw[i][:].indirect(offsets[:, 32 * b : 32 * (b + 1)]),
-            )
+        def gather_wd(i):
+            picked[i] = vector_tile([P, 2, PASS + 32], BF16)
+            nc.vector.tensor_copy(picked[i][:, :, 0:PASS], wd_raw[i][:].indirect(offsets[:]))
 
         def turn_wd(i):
             turned = bank_tile([P, 4, P])
             for b in range(2):
-                words = picked[(i, b)][:].bitcast(F32)
+                words = picked[i][:, b, 0:PASS].bitcast(F32)
                 for u in range(2):
-                    nc.tensor.transpose(turned[:, 2 * b + u, :], words[:, u * P : (u + 1) * P], ident[:])
+                    nc.tensor.transpose(turned[:, 2 * b + u, :], words[:, u : 2 * P : 2], ident[:])
             wd_grouped[i] = scalar_tile([P, S], BF16)
             nc.scalar.copy(
                 wd_grouped[i][:].bitcast(F32).rearrange("p (b n u) -> p b n u", b=2, u=2),
@@ -262,140 +272,138 @@ def tile_list_sparse_reservoir_control_kernel(tc, x, tab_words, tab_scales, offs
             nc.scalar.activation(result[:], bank[:].rearrange("p s w -> p (s w)"), ACT.Tanh, bias=c_sb[:, i : i + 1])
             nc.sync.dma_start(out[i * P : (i + 1) * P, m0 : m0 + groups * P], result[:])
 
-        load_tab(1, nc.scalar)
         load_rows(x_raw, x, 0, 0, 256)
-        load_rows(x_raw, x, 1, 256, 256, nc.scalar)
-        load_rows(x_raw, x, 1, 0, 256, nc.scalar)
+        group_x("S", 0, 0, 256)
+        load_tab(0)
+        load_tab(1)
+        gather_tab(0)
+        load_rows(x_raw, x, 1, 0, 256)
+        load_c(0, nc.scalar)
+        load_rows(x_raw, x, 1, 256, 256)
         load_rows(x_raw, x, 0, 256, 256)
         load_rows(r_sb, r, 0, 0, 256)
-        load_g(0, nc.scalar)
-        group_x("S", 0, 0, 256)
-        gather_scales()
-        load_tab(0)
         load_rows(r_sb, r, 1, 0, 256)
-        group_x("S", 1, 256, 256)
-        group_x("S", 1, 0, 256)
-        load_wfs(2)
-        gather_tab(0)
         load_wd(0)
-        group_x("S", 0, 256, 256)
-        load_rows(r_sb, r, 0, 256, 256)
-        load_rows(x_raw, x, 0, 512, 256)
         quantize_x(0, 0, 256)
-        quantize_x(1, 0, 256)
-        quantize_x(1, 256, 256)
-        turn_scales()
-        gather_tab(1)
-        add_h(0, 128)
-        add_h(0, 0)
-        add_h(1, 0)
-        add_h(1, 128)
-        make_h(0, 0, 256, "S")
-        make_h(1, 0, 256, "S")
-        scale_h(1, 0)
-        quantize_x(0, 256, 256)
-        load_rows(x_raw, x, 1, 512, 256)
-        load_rows(r_sb, r, 1, 256, 256)
-        scale_h(0, 0)
-        gather_wd(0, 1)
-        gather_wd(0, 0)
-        gain_h(1, 0)
-        add_h(0, 256)
-        group_x("S", 0, 512, 256)
-        quantize_h(1, 0)
-        gain_h(0, 0)
-        add_h(1, 384)
-        group_x("S", 1, 512, 256)
-        load_wd(1)
-        load_wfs(3)
-        add_h(0, 384)
-        quantize_x(1, 512, 256)
-        make_h(0, 256, 256, "S")
-        quantize_x(0, 512, 256)
-        add_h(1, 256)
-        gather_wd(1, 0)
-        gather_wd(1, 1)
-        load_wd(2)
-        load_rows(x_raw, x, 1, 768, 256)
         load_wfs(1)
-        load_wf()
-        turn_wd(0)
-        scale_h(0, 256)
-        make_h(1, 256, 256, "S")
-        quantize_wd(0)
-        load_rows(r_sb, r, 0, 512, 256)
-        gather_wd(2, 1)
+        load_g(0, nc.scalar)
+        load_rows(r_sb, r, 0, 256, 256)
+        group_x("S", 1, 0, 256)
+        gather_scales()
+        load_rows(r_sb, r, 1, 256, 256)
+        turn_g()
+        load_wd(1)
         load_wfs(0)
+        group_x("S", 1, 256, 256)
+        group_x("S", 0, 256, 256)
+        load_wfs(3)
+        load_rows(x_raw, x, 0, 512, 256)
+        gather_tab(1)
+        quantize_x(1, 0, 256)
+        turn_scales()
+        turn_c()
+        quantize_x(1, 256, 256)
+        quantize_x(0, 256, 256)
+        add_h(0, 128)
+        add_h(1, 0)
+        load_rows(x_raw, x, 1, 512, 256)
+        add_h(0, 0)
+        add_h(1, 128)
+        load_wd(2)
+        make_h(1, 0, 256, "S")
+        gather_wd(0)
+        scale_h(1, 0)
+        make_h(0, 0, 256, "S")
+        scale_h(0, 0)
+        add_h(0, 256)
+        load_rows(r_sb, r, 0, 512, 256)
+        add_h(1, 256)
+        add_h(1, 384)
         load_rows(x_raw, x, 0, 768, 256)
+        gain_h(1, 0)
+        load_rows(x_raw, x, 1, 768, 256)
+        add_h(0, 384)
+        make_h(0, 256, 256, "S")
+        group_x("S", 0, 512, 256)
         load_rows(r_sb, r, 1, 512, 256)
+        group_x("S", 1, 512, 256)
+        gain_h(0, 0)
+        load_wfs(2)
+        load_wf()
+        gather_wd(1)
+        quantize_h(1, 0)
         quantize_h(0, 0)
-        turn_wd(1)
-        group_x("S", 1, 768, 256)
-        gather_wd(2, 0)
+        quantize_x(1, 512, 256)
+        turn_wd(0)
+        make_h(1, 256, 256, "S")
+        scale_h(0, 256)
+        quantize_x(0, 512, 256)
+        quantize_wd(0)
+        gather_wd(2)
+        add_h(0, 512)
         gain_h(0, 256)
         scale_h(1, 256)
-        quantize_wd(1)
-        load_wd(3)
-        add_h(0, 512)
-        quantize_h(0, 256)
-        load_c(0)
-        add_h(0, 640)
-        turn_wd(2)
-        quantize_x(1, 768, 256)
-        make_h(0, 512, 256, "S")
         group_x("S", 0, 768, 256)
         gain_h(1, 256)
-        add_h(1, 512)
-        quantize_h(1, 256)
-        load_rows(r_sb, r, 0, 768, 256)
+        add_h(0, 640)
+        turn_wd(1)
+        group_x("S", 1, 768, 256)
         add_h(1, 640)
-        quantize_x(0, 768, 256)
-        quantize_wd(2)
-        gather_wd(3, 0)
+        turn_wd(2)
+        add_h(1, 512)
+        quantize_h(0, 256)
+        load_wd(3)
         make_h(1, 512, 256, "S")
+        quantize_h(1, 256)
+        quantize_wd(1)
+        load_rows(r_sb, r, 0, 768, 256)
         load_rows(r_sb, r, 1, 768, 256)
-        scale_h(0, 512)
-        make_y(0, 0, 128, 4)
-        make_y(1, 0, 128, 4)
-        gather_wd(3, 1)
-        add_h(0, 768)
         scale_h(1, 512)
-        add_h(1, 896)
-        add_h(1, 768)
+        make_h(0, 512, 256, "S")
+        quantize_wd(2)
+        make_y(0, 0, 128, 4)
+        quantize_x(0, 768, 256)
+        scale_h(0, 512)
+        quantize_x(1, 768, 256)
+        gather_wd(3)
+        gain_h(1, 512)
+        make_y(1, 0, 128, 4)
+        add_h(0, 768)
         add_h(0, 896)
+        add_h(1, 768)
         turn_wd(3)
         make_h(1, 768, 128, "V")
-        quantize_wd(3)
         make_h(0, 768, 128, "V")
-        gain_h(0, 512)
-        make_h(0, 896, 128, "S")
-        make_y(2, 0, 128, 4)
-        scale_h(0, 896)
         scale_h(1, 768)
-        make_h(1, 896, 128, "V")
-        scale_h(1, 896)
+        add_h(1, 896)
+        quantize_wd(3)
+        make_h(0, 896, 128, "V")
         scale_h(0, 768)
-        gain_h(1, 512)
-        quantize_h(0, 512)
+        make_h(1, 896, 128, "V")
+        gain_h(0, 512)
+        scale_h(0, 896)
         quantize_h(1, 512)
-        gain_h(1, 768)
-        make_y(3, 0, 128, 4)
-        open_y(2, 896)
+        scale_h(1, 896)
+        make_y(2, 0, 128, 4)
+        quantize_h(0, 512)
         gain_h(0, 768)
-        quantize_h(1, 768)
-        open_y(1, 896)
+        gain_h(1, 768)
         quantize_h(0, 768)
-        open_y(0, 896)
+        quantize_h(1, 768)
+        make_y(3, 0, 128, 4)
         gain_h(1, 896)
-        make_y(2, 512, 128, 3)
-        gain_h(0, 896)
-        make_y(1, 512, 128, 3)
-        quantize_h(1, 896)
-        quantize_h(0, 896)
         make_y(3, 512, 128, 3)
-        open_y(3, 896)
-        make_y(3, 896, 128, 1)
+        open_y(2, 896)
+        gain_h(0, 896)
+        quantize_h(0, 896)
+        make_y(1, 512, 128, 3)
+        open_y(1, 896)
+        quantize_h(1, 896)
+        make_y(2, 512, 128, 3)
         make_y(0, 512, 128, 3)
+        open_y(0, 896)
+        open_y(3, 896)
         make_y(0, 896, 128, 1)
         make_y(1, 896, 128, 1)
+        make_y(3, 896, 128, 1)
         make_y(2, 896, 128, 1)

@@ -20,8 +20,17 @@ ALU = mybir.AluOpType
 P = 128
 PACK = 4
 PASS = P * PACK
-BANK = 512
-HALF = 512
+CHUNK = 256
+LAST = M - P
+GAIN_RUN = 64
+PAD = 32
+
+VECTOR_SLOTS = 48
+SCALAR_SLOTS = 9
+GPSIMD_SLOTS = 3
+TABLE_SLOTS = 3
+ROWS_SLOTS = 10
+PSUM_BANKS = 8
 
 
 def tile_list_sparse_reservoir_control_kernel(tc, x, tab_words, tab_scales, offs, r, g, wdT, wf_words, wf_scales, c, out):
@@ -29,13 +38,16 @@ def tile_list_sparse_reservoir_control_kernel(tc, x, tab_words, tab_scales, offs
     with ExitStack() as ctx:
         keep = ctx.enter_context(tc.tile_pool(name="keep", bufs=1))
         ring = ctx.enter_context(tc.tile_pool(name="ring", bufs=1))
-        psum = ctx.enter_context(tc.psum_pool(name="psum", bufs=8))
+        psum = ctx.enter_context(tc.psum_pool(name="psum", bufs=PSUM_BANKS))
 
         def vector_tile(shape, dtype):
-            return ring.tile(shape, dtype, name="vector_out", align_bytes=64, bufs=50)
+            return ring.tile(shape, dtype, name="vector_out", align_bytes=64, bufs=VECTOR_SLOTS)
 
         def scalar_tile(shape, dtype):
-            return ring.tile(shape, dtype, name="scalar_out", align_bytes=64, bufs=10)
+            return ring.tile(shape, dtype, name="scalar_out", align_bytes=64, bufs=SCALAR_SLOTS)
+
+        def gpsimd_tile(shape, dtype):
+            return ring.tile(shape, dtype, name="gpsimd_out", align_bytes=64, bufs=GPSIMD_SLOTS)
 
         def bank_tile(shape):
             return psum.tile(shape, F32, name="bank")
@@ -47,12 +59,8 @@ def tile_list_sparse_reservoir_control_kernel(tc, x, tab_words, tab_scales, offs
         nc.vector.memset(tab_plane[:], 0)
         wf_plane = keep.tile([P, 2, N // 4], I32, name="wf_plane", align_bytes=64)
         nc.gpsimd.memset(wf_plane[:], 0)
-        warm = keep.tile([P, 8], F32, name="warm")
-        nc.vector.memset(warm[:], 0.0)
         for q in range(4):
             nc.sync.dma_start(tab_plane[32 * q : 32 * q + 8, :], tab_scales[:, 4 * q : 4 * q + 4, :].bitcast(I32))
-        warm_out = keep.tile([P, 8], F32, name="warm_out")
-        nc.scalar.activation(warm_out[:], warm[:], ACT.Tanh)
         ident = keep.tile([P, P], F32, name="ident", align_bytes=64)
         make_identity(nc, ident[:])
 
@@ -60,350 +68,384 @@ def tile_list_sparse_reservoir_control_kernel(tc, x, tab_words, tab_scales, offs
         vectors = keep.tile([P, PASS], F32, name="vectors", align_bytes=64)
         nc.gpsimd.memset(vectors[:], 0.0)
         g_sb = keep.tile([P, 2, PACK], F32, name="g_sb")
+        g_wide = keep.tile([P, 2, GAIN_RUN * PACK], F32, name="g_wide", align_bytes=64)
         c_sb = keep.tile([P, N // P], F32, name="c_sb")
         v_codes = [keep.tile([P, S], U32, name=f"v_codes{a}", align_bytes=64) for a in range(2)]
         v_plane_list = keep.tile([P, S], U8, name="v_plane_list", align_bytes=64)
         v_plane = keep.tile([P, S], U8, name="v_plane", align_bytes=64)
+
         tab, wd_raw, x_raw, r_sb = {}, {}, {}, {}
-        x_grouped, x_mx, h_mx, wd_mx = {}, {}, {}, {}
-        staged, gained, picked, wd_grouped = {}, {}, {}, {}
+        x_grouped, h_grouped, wd_picked, wd_grouped = {}, {}, {}, {}
+        x_mx, h_mx, wd_mx = {}, {}, {}
+        summed, squashed, gained_rows, last_banks = {}, {}, {}, {}
 
-        def load_tab(a, queue=nc.sync):
-            tab[a] = ring.tile([P, T], I32, name="table", align_bytes=64, bufs=3)
-            queue.dma_start(tab[a][:], tab_words[a].rearrange("p t i -> p (t i)").bitcast(I32))
 
-        def load_wd(i, queue=nc.sync):
-            wd_raw[i] = ring.tile([P, T], F32, name="table", align_bytes=64, bufs=3)
-            queue.dma_start(wd_raw[i][:], wdT[i * P : (i + 1) * P, :])
+        def load_table(a):
+            tab[a] = ring.tile([P, T], I32, name="table", align_bytes=64, bufs=TABLE_SLOTS)
+            nc.sync.dma_start(tab[a][:], tab_words[a].rearrange("p t i -> p (t i)").bitcast(I32))
 
-        def load_rows(dst, src, a, m0, w, queue=nc.sync):
-            rows = src[a * PASS : (a + 1) * PASS, m0 : m0 + w]
-            dst[(a, m0)] = ring.tile([P, PACK, w], F32, name="rows", align_bytes=64, bufs=10)
-            queue.dma_start(dst[(a, m0)][:], rows.rearrange("(p t) m -> p t m", t=PACK))
+        def load_readout(i):
+            wd_raw[i] = ring.tile([P, T], F32, name="table", align_bytes=64, bufs=TABLE_SLOTS)
+            nc.sync.dma_start(wd_raw[i][:], wdT[i * P : (i + 1) * P, :])
 
-        def load_wf(queue=nc.sync):
-            queue.dma_start(wf[:], wf_words.bitcast(I32).rearrange("a p e -> p a e"))
+        def load_rows(src, half, m0):
+            rows = ring.tile([P, PACK, CHUNK], F32, name="rows", align_bytes=64, bufs=ROWS_SLOTS)
+            part = src[half * PASS : (half + 1) * PASS, m0 : m0 + CHUNK]
+            nc.sync.dma_start(rows[:], part.rearrange("(p t) m -> p t m", t=PACK))
+            return rows
 
-        def load_wfs(row, queue=nc.sync):
-            queue.dma_start(wf_plane[row:P:32, :, :], wf_scales.bitcast(I32)[:, row:16:4, :].rearrange("a q e -> q a e"))
+        def load_x(a, m0):
+            x_raw[(a, m0)] = load_rows(x, a, m0)
 
-        def load_c(unused, queue=nc.sync):
-            queue.dma_start(vectors[2:3, :], c.rearrange("(o n) -> o n", o=1))
+        def load_r(b, m0):
+            r_sb[(b, m0)] = load_rows(r, b, m0)
 
-        def turn_c():
-            turned = bank_tile([P, 4, P])
+        def load_direct_words():
+            nc.sync.dma_start(wf[:], wf_words.bitcast(I32).rearrange("a p e -> p a e"))
+
+        def load_direct_scales(s):
+            nc.sync.dma_start(wf_plane[s:P:32, :, :], wf_scales.bitcast(I32)[:, s:16:4, :].rearrange("a q e -> q a e"))
+
+        def load_biases():
+            nc.scalar.dma_start(vectors[2:3, :], c.rearrange("(o n) -> o n", o=1))
+
+        def load_gains():
+            nc.scalar.dma_start(vectors[0:2, :], g.rearrange("(b j) -> b j", b=2))
+
+        def turn_biases():
+            turned = bank_tile([P, N // P, P])
             for i in range(N // P):
                 nc.tensor.transpose(turned[:, i, :], vectors[:, i * P : (i + 1) * P], ident[:])
             nc.scalar.copy(c_sb[:], turned[:, :, 2])
 
-        def turn_g():
-            turned = bank_tile([P, 4, P])
+        def turn_gains():
+            turned = bank_tile([P, PACK, P])
             for t in range(PACK):
                 nc.tensor.transpose(turned[:, t, :], vectors[:, t:PASS:PACK], ident[:])
             nc.scalar.copy(g_sb[:], turned[:, :, 0:2].rearrange("p t b -> p b t"))
+            nc.scalar.copy(
+                g_wide[:].rearrange("p b (m t) -> p b m t", t=PACK),
+                g_sb[:].rearrange("p b (o t) -> p b o t", o=1).to_broadcast([P, 2, GAIN_RUN, PACK]),
+            )
 
-        def load_g(unused, queue=nc.sync):
-            queue.dma_start(vectors[0:2, :], g.rearrange("(b j) -> b j", b=2))
 
-        def gather_tab(a):
+        def gather_table_words(a):
             nc.vector.tensor_copy(
                 v_codes[a][:].rearrange("k (b t p) -> k b p t", b=2, t=PACK),
                 tab[a][:].bitcast(U32).indirect(offsets[:]),
             )
 
-        def gather_scales():
+        def gather_table_scales():
             nc.vector.tensor_copy(v_plane_list[:], tab_plane[:].bitcast(U8).indirect(offsets[:]))
 
-        def turn_scales():
+        def order_table_scales():
             nc.vector.tensor_copy(
                 v_plane[:].rearrange("k (b t p) -> k b t p", b=2, t=PACK),
                 v_plane_list[:].rearrange("k (b p t) -> k b t p", b=2, t=PACK),
             )
 
-        def quantize(values, width):
+
+        def quantize(grouped, width):
             mx = vector_tile([P, 5 * width], U8)
-            nc.vector.quantize_mx(out=mx[:, 0 : 4 * width].bitcast(FP8X4), scales=mx[:, 4 * width : 5 * width], in_=values)
+            nc.vector.quantize_mx(out=mx[:, 0 : 4 * width].bitcast(FP8X4), scales=mx[:, 4 * width : 5 * width], in_=grouped)
             return mx, width
 
-        def operand(mx_width, start):
-            mx, width = mx_width
-            return mx[:, 4 * start : 4 * (start + P)].bitcast(FP8X4), mx[:, 4 * width + start : 4 * width + start + P]
+        def operand(quantized, first):
+            mx, width = quantized
+            return mx[:, 4 * first : 4 * (first + P)].bitcast(FP8X4), mx[:, 4 * width + first : 4 * width + first + P]
 
-        def columns(tiles, a, m0):
-            start = max(key[1] for key in tiles if key[0] == a and key[1] <= m0)
-            return operand(tiles[(a, start)], m0 - start)
+        def columns(tiles, half, m0):
+            start = max(key[1] for key in tiles if key[0] == half and key[1] <= m0)
+            return operand(tiles[(half, start)], m0 - start)
 
-        def group_x(engine, a, m0, w):
-            src = x_raw[(a, m0)][:].rearrange("p t (c i) -> p c t i", i=4)
-            if engine == "S":
-                x_grouped[(a, m0)] = scalar_tile([P, w, PACK], BF16)
-                nc.scalar.copy(x_grouped[(a, m0)][:].rearrange("p (c i) t -> p c t i", i=4), src)
-            else:
-                x_grouped[(a, m0)] = vector_tile([P, w, PACK], BF16)
-                nc.vector.tensor_copy(x_grouped[(a, m0)][:].rearrange("p (c i) t -> p c t i", i=4), src)
+        def as_grouped(tile):
+            return tile[:].rearrange("p (e i) t -> p e t i", i=4)
 
-        def quantize_x(a, m0, w):
-            x_mx[(a, m0)] = quantize(x_grouped[(a, m0)][:].rearrange("p m t -> p (m t)"), w)
+        def as_rows(tile):
+            return tile[:].rearrange("p t (e i) -> p e t i", i=4)
 
-        summed = {}
+        def group_x_on_scalar(a, m0):
+            x_grouped[(a, m0)] = scalar_tile([P, CHUNK, PACK], BF16)
+            nc.scalar.copy(as_grouped(x_grouped[(a, m0)]), as_rows(x_raw[(a, m0)]))
 
-        def add_h(b, m1):
+        def group_x_on_vector(a, m0):
+            x_grouped[(a, m0)] = vector_tile([P, CHUNK, PACK], BF16)
+            nc.vector.tensor_copy(as_grouped(x_grouped[(a, m0)]), as_rows(x_raw[(a, m0)]))
+
+        def quantize_x(a, m0):
+            x_mx[(a, m0)] = quantize(x_grouped[(a, m0)][:].rearrange("p m t -> p (m t)"), CHUNK)
+
+
+        def project(b, m0):
             bank = bank_tile([P, PACK, P])
             for t in range(PACK):
-                jcols = slice(b * PASS + t * P, b * PASS + (t + 1) * P)
+                picks = slice(b * PASS + t * P, b * PASS + (t + 1) * P)
                 for a in range(2):
-                    codes, plane = columns(x_mx, a, m1)
+                    codes, plane = columns(x_mx, a, m0)
                     nc.tensor.matmul_mx(
                         out=bank[:, t, :],
-                        lhsT=v_codes[a][:, jcols].bitcast(FP8X4),
-                        lhsT_scale=v_plane[4 * a : P, jcols],
+                        lhsT=v_codes[a][:, picks].bitcast(FP8X4),
+                        lhsT_scale=v_plane[4 * a : P, picks],
                         rhs=codes,
                         rhs_scale=plane,
                         start=(a == 0),
                         stop=(a == 1),
                     )
-            z = vector_tile([P, PACK, P], F32)
-            start = m1 // 256 * 256
-            nc.vector.tensor_tensor(z[:], bank[:], r_sb[(b, start)][:, :, m1 - start : m1 - start + P], ALU.add)
-            summed[(b, m1)] = z
+            summed[(b, m0)] = vector_tile([P, PACK, P], F32)
+            start = m0 // CHUNK * CHUNK
+            drive = r_sb[(b, start)][:, :, m0 - start : m0 - start + P]
+            nc.vector.tensor_tensor(summed[(b, m0)][:], bank[:], drive, ALU.add)
 
-        def make_h(b, m0, w, mode):
-            th = scalar_tile([P, w // P, PACK * P], F32)
-            for m1 in range(m0, m0 + w, P):
-                z = summed[(b, m1)]
-                part = th[:, (m1 - m0) // P, :]
-                if mode == "S":
-                    nc.scalar.activation(part, z[:].rearrange("p t m -> p (t m)"), ACT.Tanh)
-                else:
-                    nc.scalar.activation(
-                        part.rearrange("p (c i t) -> p c t i", i=4, t=PACK),
-                        z[:].rearrange("p t (c i) -> p c t i", i=4),
-                        ACT.Tanh,
-                    )
-            staged[(b, m0)] = (th, mode, w)
 
-        def scale_h(b, m0):
-            th, mode, w = staged[(b, m0)]
-            if mode == "S":
-                slots = scalar_tile([P, PACK, w], BF16)
-                for t in range(PACK):
-                    nc.scalar.activation(
-                        slots[:, t, :].rearrange("p (s m) -> p s m", m=P),
-                        th[:, :, t * P : (t + 1) * P],
-                        ACT.Copy,
-                        scale=g_sb[:, b, t : t + 1],
-                    )
-                staged[(b, m0)] = (slots, mode, w)
-
-        def gain_h(b, m0):
-            th, mode, w = staged[(b, m0)]
-            hb = vector_tile([P, w, PACK], BF16)
-            if mode == "S":
-                nc.vector.tensor_copy(hb[:].rearrange("p (c i) t -> p c t i", i=4), th[:].rearrange("p t (c i) -> p c t i", i=4))
-            else:
-                nc.vector.tensor_tensor(
-                    hb[:],
-                    th[:].rearrange("p s (m t) -> p (s m) t", t=PACK),
-                    g_sb[:, b : b + 1, :].to_broadcast([P, w, PACK]),
-                    ALU.mult,
+        def tanh_grouped(b, m0, width):
+            squashed[(b, m0)] = scalar_tile([P, width // P, PACK * P], F32)
+            for s in range(width // P):
+                nc.scalar.activation(
+                    squashed[(b, m0)][:, s, :].rearrange("p (e i t) -> p e t i", i=4, t=PACK),
+                    as_rows(summed[(b, m0 + s * P)]),
+                    ACT.Tanh,
                 )
-            gained[(b, m0)] = (hb, w)
+
+        def gain_on_vector(b, m0):
+            h_grouped[(b, m0)] = vector_tile([P, P, PACK], BF16)
+            nc.vector.tensor_tensor(
+                h_grouped[(b, m0)][:],
+                squashed[(b, m0)][:].rearrange("p s (m t) -> p (s m) t", t=PACK),
+                g_sb[:, b : b + 1, :].to_broadcast([P, P, PACK]),
+                ALU.mult,
+            )
+
+        def gain_on_gpsimd(b, m0):
+            h_grouped[(b, m0)] = gpsimd_tile([P, CHUNK, PACK], BF16)
+            nc.gpsimd.tensor_tensor(
+                h_grouped[(b, m0)][:].rearrange("p (s m) t -> p s (m t)", m=GAIN_RUN),
+                squashed[(b, m0)][:].rearrange("p s (h e) -> p (s h) e", e=GAIN_RUN * PACK),
+                g_wide[:, b : b + 1, :].to_broadcast([P, CHUNK // GAIN_RUN, GAIN_RUN * PACK]),
+                ALU.mult,
+            )
+
+        def tanh_by_rows(b, m0, width):
+            squashed[(b, m0)] = scalar_tile([P, width // P, PACK * P], F32)
+            for s in range(width // P):
+                nc.scalar.activation(squashed[(b, m0)][:, s, :], summed[(b, m0 + s * P)][:].rearrange("p t m -> p (t m)"), ACT.Tanh)
+
+        def gain_on_scalar(b, m0):
+            gained_rows[(b, m0)] = scalar_tile([P, PACK, CHUNK], BF16)
+            for t in range(PACK):
+                nc.scalar.activation(
+                    gained_rows[(b, m0)][:, t, :].rearrange("p (s m) -> p s m", m=P),
+                    squashed[(b, m0)][:, :, t * P : (t + 1) * P],
+                    ACT.Copy,
+                    scale=g_sb[:, b, t : t + 1],
+                )
+
+        def group_h(b, m0):
+            h_grouped[(b, m0)] = vector_tile([P, CHUNK, PACK], BF16)
+            nc.vector.tensor_copy(as_grouped(h_grouped[(b, m0)]), as_rows(gained_rows[(b, m0)]))
 
         def quantize_h(b, m0):
-            hb, w = gained[(b, m0)]
-            h_mx[(b, m0)] = quantize(hb[:].rearrange("p m t -> p (m t)"), w)
+            grouped = h_grouped[(b, m0)]
+            h_mx[(b, m0)] = quantize(grouped[:].rearrange("p m t -> p (m t)"), grouped[:].shape[1])
 
-        def gather_wd(i):
-            picked[i] = vector_tile([P, 2, PASS + 32], BF16)
-            nc.vector.tensor_copy(picked[i][:, :, 0:PASS], wd_raw[i][:].indirect(offsets[:]))
 
-        def turn_wd(i):
+        def gather_readout(i):
+            wd_picked[i] = vector_tile([P, 2, PASS + PAD], BF16)
+            nc.vector.tensor_copy(wd_picked[i][:, :, 0:PASS], wd_raw[i][:].indirect(offsets[:]))
+
+        def turn_readout(i):
             turned = bank_tile([P, 4, P])
             for b in range(2):
-                words = picked[i][:, b, 0:PASS].bitcast(F32)
+                pairs = wd_picked[i][:, b, 0:PASS].bitcast(F32)
                 for u in range(2):
-                    nc.tensor.transpose(turned[:, 2 * b + u, :], words[:, u : 2 * P : 2], ident[:])
+                    nc.tensor.transpose(turned[:, 2 * b + u, :], pairs[:, u : 2 * P : 2], ident[:])
             wd_grouped[i] = scalar_tile([P, S], BF16)
             nc.scalar.copy(
                 wd_grouped[i][:].bitcast(F32).rearrange("p (b n u) -> p b n u", b=2, u=2),
                 turned[:].rearrange("p (b u) n -> p b n u", b=2),
             )
 
-        def quantize_wd(i):
+        def quantize_readout(i):
             wd_mx[i] = quantize(wd_grouped[i][:], 2 * P)
 
-        opened = {}
 
-        def open_y(i, m0):
-            make_y(i, m0, P, 1, True)
+        def direct_passes(group, i, m0):
+            for a in range(2):
+                codes, plane = columns(x_mx, a, m0)
+                nc.tensor.matmul_mx(
+                    out=group,
+                    lhsT=wf[:, a, :].bitcast(U8)[:, 2 * i * P : 2 * (i + 1) * P].bitcast(FP4X4),
+                    lhsT_scale=wf_plane[:, a, :].bitcast(U8)[:, i * P : (i + 1) * P],
+                    rhs=codes,
+                    rhs_scale=plane,
+                    start=(a == 0),
+                    stop=False,
+                )
 
-        def make_y(i, m0, w, groups, only_open=False):
-            fresh = (i, m0) not in opened
-            if fresh:
-                opened[(i, m0)] = bank_tile([P, groups, P])
-            bank = opened[(i, m0)]
-            for s in range(groups):
-                for a in range(2 if fresh else 0):
-                    codes, plane = columns(x_mx, a, m0 + s * P)
-                    nc.tensor.matmul_mx(
-                        out=bank[:, s, :],
-                        lhsT=wf[:, a, :].bitcast(U8)[:, 2 * i * P : 2 * (i + 1) * P].bitcast(FP4X4),
-                        lhsT_scale=wf_plane[:, a, :].bitcast(U8)[:, i * P : (i + 1) * P],
-                        rhs=codes,
-                        rhs_scale=plane,
-                        start=(a == 0),
-                        stop=False,
-                    )
-                if only_open:
-                    return
-                for b in range(2):
-                    codes, plane = columns(h_mx, b, m0 + s * P)
-                    weights, weight_plane = operand(wd_mx[i], b * P)
-                    nc.tensor.matmul_mx(
-                        out=bank[:, s, :],
-                        lhsT=weights,
-                        lhsT_scale=weight_plane,
-                        rhs=codes,
-                        rhs_scale=plane,
-                        start=False,
-                        stop=(b == 1),
-                    )
+        def readout_passes(group, i, m0):
+            for b in range(2):
+                codes, plane = columns(h_mx, b, m0)
+                weights, weight_plane = operand(wd_mx[i], b * P)
+                nc.tensor.matmul_mx(
+                    out=group,
+                    lhsT=weights,
+                    lhsT_scale=weight_plane,
+                    rhs=codes,
+                    rhs_scale=plane,
+                    start=False,
+                    stop=(b == 1),
+                )
+
+        def saturate_and_store(bank, i, m0, groups):
             result = scalar_tile([P, groups * P], F32)
             nc.scalar.activation(result[:], bank[:].rearrange("p s w -> p (s w)"), ACT.Tanh, bias=c_sb[:, i : i + 1])
             nc.sync.dma_start(out[i * P : (i + 1) * P, m0 : m0 + groups * P], result[:])
 
-        load_rows(x_raw, x, 0, 0, 256)
-        group_x("S", 0, 0, 256)
-        load_tab(0)
-        load_tab(1)
-        gather_tab(0)
-        load_rows(x_raw, x, 1, 0, 256)
-        load_c(0, nc.scalar)
-        load_rows(x_raw, x, 1, 256, 256)
-        load_rows(x_raw, x, 0, 256, 256)
-        load_rows(r_sb, r, 0, 0, 256)
-        load_rows(r_sb, r, 1, 0, 256)
-        load_wd(0)
-        quantize_x(0, 0, 256)
-        load_wfs(1)
-        load_g(0, nc.scalar)
-        load_rows(r_sb, r, 0, 256, 256)
-        group_x("S", 1, 0, 256)
-        gather_scales()
-        load_rows(r_sb, r, 1, 256, 256)
-        turn_g()
-        load_wd(1)
-        load_wfs(0)
-        group_x("S", 1, 256, 256)
-        group_x("S", 0, 256, 256)
-        load_wfs(3)
-        load_rows(x_raw, x, 0, 512, 256)
-        gather_tab(1)
-        quantize_x(1, 0, 256)
-        turn_scales()
-        turn_c()
-        quantize_x(1, 256, 256)
-        quantize_x(0, 256, 256)
-        add_h(0, 128)
-        add_h(1, 0)
-        load_rows(x_raw, x, 1, 512, 256)
-        add_h(0, 0)
-        add_h(1, 128)
-        load_wd(2)
-        make_h(1, 0, 256, "S")
-        gather_wd(0)
-        scale_h(1, 0)
-        make_h(0, 0, 256, "S")
-        scale_h(0, 0)
-        add_h(0, 256)
-        load_rows(r_sb, r, 0, 512, 256)
-        add_h(1, 256)
-        add_h(1, 384)
-        load_rows(x_raw, x, 0, 768, 256)
-        gain_h(1, 0)
-        load_rows(x_raw, x, 1, 768, 256)
-        add_h(0, 384)
-        make_h(0, 256, 256, "S")
-        group_x("S", 0, 512, 256)
-        load_rows(r_sb, r, 1, 512, 256)
-        group_x("S", 1, 512, 256)
-        gain_h(0, 0)
-        load_wfs(2)
-        load_wf()
-        gather_wd(1)
+        def commands(i, m0, groups):
+            bank = bank_tile([P, groups, P])
+            for s in range(groups):
+                direct_passes(bank[:, s, :], i, m0 + s * P)
+                readout_passes(bank[:, s, :], i, m0 + s * P)
+            saturate_and_store(bank, i, m0, groups)
+
+
+        def open_last_commands(i):
+            last_banks[i] = bank_tile([P, 1, P])
+            direct_passes(last_banks[i][:, 0, :], i, LAST)
+
+        def close_last_commands(i):
+            readout_passes(last_banks[i][:, 0, :], i, LAST)
+            saturate_and_store(last_banks[i], i, LAST, 1)
+
+
+        load_x(0, 0)
+        load_table(1)
+        group_x_on_scalar(0, 0)
+        load_x(1, 0)
+        gather_table_scales()
+        load_table(0)
+        group_x_on_scalar(1, 0)
+        load_x(1, 256)
+        load_biases()
+        load_x(0, 256)
+        quantize_x(0, 0)
+        load_r(1, 0)
+        group_x_on_scalar(1, 256)
+        quantize_x(1, 256)
+        quantize_x(1, 0)
+        load_r(0, 0)
+        load_readout(0)
+        load_r(1, 256)
+        load_gains()
+        order_table_scales()
+        turn_biases()
+        group_x_on_vector(0, 256)
+        gather_table_words(0)
+        turn_gains()
+        gather_table_words(1)
+        load_x(0, 512)
+        quantize_x(0, 256)
+        load_r(0, 256)
+        load_readout(1)
+        load_direct_scales(1)
+        load_direct_scales(0)
+
+        project(0, 0)
+        project(1, 0)
+        project(1, 128)
+        tanh_by_rows(1, 0, 256)
+        project(0, 128)
+        tanh_grouped(0, 0, 256)
+        load_x(1, 512)
+        gain_on_scalar(1, 0)
+        gather_readout(0)
+        group_x_on_scalar(0, 512)
+        project(1, 256)
+        load_direct_scales(3)
+        project(1, 384)
+        project(0, 384)
+        load_readout(2)
+        project(0, 256)
+        turn_readout(0)
+        group_x_on_scalar(1, 512)
+        load_r(1, 512)
+        load_direct_scales(2)
+        group_h(1, 0)
+        tanh_grouped(1, 256, 256)
+        gather_readout(1)
+        quantize_x(0, 512)
+        load_x(0, 768)
+        quantize_readout(0)
+        load_r(0, 512)
+        load_direct_words()
         quantize_h(1, 0)
+        quantize_x(1, 512)
+        gain_on_gpsimd(0, 0)
         quantize_h(0, 0)
-        quantize_x(1, 512, 256)
-        turn_wd(0)
-        make_h(1, 256, 256, "S")
-        scale_h(0, 256)
-        quantize_x(0, 512, 256)
-        quantize_wd(0)
-        gather_wd(2)
-        add_h(0, 512)
-        gain_h(0, 256)
-        scale_h(1, 256)
-        group_x("S", 0, 768, 256)
-        gain_h(1, 256)
-        add_h(0, 640)
-        turn_wd(1)
-        group_x("S", 1, 768, 256)
-        add_h(1, 640)
-        turn_wd(2)
-        add_h(1, 512)
-        quantize_h(0, 256)
-        load_wd(3)
-        make_h(1, 512, 256, "S")
+
+        gather_readout(2)
+        project(1, 640)
+        tanh_by_rows(0, 256, 256)
+        gain_on_scalar(0, 256)
+        project(1, 512)
+        gain_on_gpsimd(1, 256)
+        project(0, 512)
+        project(0, 640)
+        load_x(1, 768)
+        group_h(0, 256)
+        turn_readout(1)
+        quantize_readout(1)
+        group_x_on_scalar(0, 768)
+        load_readout(3)
+        quantize_x(0, 768)
+        turn_readout(2)
         quantize_h(1, 256)
-        quantize_wd(1)
-        load_rows(r_sb, r, 0, 768, 256)
-        load_rows(r_sb, r, 1, 768, 256)
-        scale_h(1, 512)
-        make_h(0, 512, 256, "S")
-        quantize_wd(2)
-        make_y(0, 0, 128, 4)
-        quantize_x(0, 768, 256)
-        scale_h(0, 512)
-        quantize_x(1, 768, 256)
-        gather_wd(3)
-        gain_h(1, 512)
-        make_y(1, 0, 128, 4)
-        add_h(0, 768)
-        add_h(0, 896)
-        add_h(1, 768)
-        turn_wd(3)
-        make_h(1, 768, 128, "V")
-        make_h(0, 768, 128, "V")
-        scale_h(1, 768)
-        add_h(1, 896)
-        quantize_wd(3)
-        make_h(0, 896, 128, "V")
-        scale_h(0, 768)
-        make_h(1, 896, 128, "V")
-        gain_h(0, 512)
-        scale_h(0, 896)
+        group_x_on_scalar(1, 768)
+        load_r(1, 768)
+        tanh_grouped(1, 512, 256)
+        quantize_h(0, 256)
+        tanh_by_rows(0, 512, 256)
+        quantize_readout(2)
+
+        commands(0, 0, 4)
+        quantize_x(1, 768)
+        gain_on_gpsimd(1, 512)
+        gather_readout(3)
+        commands(1, 0, 4)
+        project(1, 896)
+        gain_on_scalar(0, 512)
+        load_r(0, 768)
+        project(0, 896)
+        project(0, 768)
+        project(1, 768)
+        turn_readout(3)
+        quantize_readout(3)
+
+        tanh_grouped(0, 768, 128)
+        tanh_grouped(1, 768, 128)
+        group_h(0, 512)
+        tanh_grouped(0, 896, 128)
         quantize_h(1, 512)
-        scale_h(1, 896)
-        make_y(2, 0, 128, 4)
         quantize_h(0, 512)
-        gain_h(0, 768)
-        gain_h(1, 768)
+        tanh_grouped(1, 896, 128)
+        gain_on_vector(0, 768)
+        commands(3, 0, 4)
+        gain_on_vector(1, 768)
+        commands(2, 0, 4)
+        open_last_commands(0)
         quantize_h(0, 768)
         quantize_h(1, 768)
-        make_y(3, 0, 128, 4)
-        gain_h(1, 896)
-        make_y(3, 512, 128, 3)
-        open_y(2, 896)
-        gain_h(0, 896)
-        quantize_h(0, 896)
-        make_y(1, 512, 128, 3)
-        open_y(1, 896)
+        gain_on_vector(1, 896)
+        commands(0, 512, 3)
+        gain_on_vector(0, 896)
+        commands(1, 512, 3)
         quantize_h(1, 896)
-        make_y(2, 512, 128, 3)
-        make_y(0, 512, 128, 3)
-        open_y(0, 896)
-        open_y(3, 896)
-        make_y(0, 896, 128, 1)
-        make_y(1, 896, 128, 1)
-        make_y(3, 896, 128, 1)
-        make_y(2, 896, 128, 1)
+        commands(2, 512, 3)
+        quantize_h(0, 896)
+        commands(3, 512, 3)
+        open_last_commands(2)
+        open_last_commands(3)
+        open_last_commands(1)
+        close_last_commands(1)
+        close_last_commands(2)
+        close_last_commands(0)
+        close_last_commands(3)

from contextlib import ExitStack

import concourse.mybir as mybir
from concourse.masks import make_identity

K, T, S, M, N = 1024, 2048, 1024, 1024, 512
FLOPS = 2 * S * K * M + 2 * N * S * M + 2 * N * K * M

F32 = mybir.dt.float32
BF16 = mybir.dt.bfloat16
I32 = mybir.dt.int32
U32 = mybir.dt.uint32
U16 = mybir.dt.uint16
U8 = mybir.dt.uint8
FP8X4 = mybir.dt.float8_e4m3fn_x4
FP4X4 = mybir.dt.float4_e2m1fn_x4
ACT = mybir.ActivationFunctionType
ALU = mybir.AluOpType

P = 128
PACK = 4
PASS = P * PACK
CHUNK = 256
LAST = M - P
GAIN_RUN = 64
PAD = 32

VECTOR_SLOTS = 48
SCALAR_SLOTS = 9
GPSIMD_SLOTS = 3
TABLE_SLOTS = 3
ROWS_SLOTS = 10
PSUM_BANKS = 8


def tile_list_sparse_reservoir_control_kernel(tc, x, tab_words, tab_scales, offs, r, g, wdT, wf_words, wf_scales, c, out):
    nc = tc.nc
    with ExitStack() as ctx:
        keep = ctx.enter_context(tc.tile_pool(name="keep", bufs=1))
        ring = ctx.enter_context(tc.tile_pool(name="ring", bufs=1))
        psum = ctx.enter_context(tc.psum_pool(name="psum", bufs=PSUM_BANKS))

        def vector_tile(shape, dtype):
            return ring.tile(shape, dtype, name="vector_out", align_bytes=64, bufs=VECTOR_SLOTS)

        def scalar_tile(shape, dtype):
            return ring.tile(shape, dtype, name="scalar_out", align_bytes=64, bufs=SCALAR_SLOTS)

        def gpsimd_tile(shape, dtype):
            return ring.tile(shape, dtype, name="gpsimd_out", align_bytes=64, bufs=GPSIMD_SLOTS)

        def bank_tile(shape):
            return psum.tile(shape, F32, name="bank")

        offsets = keep.tile([P, S // 16], U16, name="offsets")
        nc.sync.dma_start(offsets[:], offs)

        tab_plane = keep.tile([P, T // 4], I32, name="tab_plane", align_bytes=64)
        nc.vector.memset(tab_plane[:], 0)
        wf_plane = keep.tile([P, 2, N // 4], I32, name="wf_plane", align_bytes=64)
        nc.gpsimd.memset(wf_plane[:], 0)
        for q in range(4):
            nc.sync.dma_start(tab_plane[32 * q : 32 * q + 8, :], tab_scales[:, 4 * q : 4 * q + 4, :].bitcast(I32))
        ident = keep.tile([P, P], F32, name="ident", align_bytes=64)
        make_identity(nc, ident[:])

        wf = keep.tile([P, 2, 2 * N // 4], I32, name="wf", align_bytes=64)
        vectors = keep.tile([P, PASS], F32, name="vectors", align_bytes=64)
        nc.gpsimd.memset(vectors[:], 0.0)
        g_sb = keep.tile([P, 2, PACK], F32, name="g_sb")
        g_wide = keep.tile([P, 2, GAIN_RUN * PACK], F32, name="g_wide", align_bytes=64)
        c_sb = keep.tile([P, N // P], F32, name="c_sb")
        v_codes = [keep.tile([P, S], U32, name=f"v_codes{a}", align_bytes=64) for a in range(2)]
        v_plane_list = keep.tile([P, S], U8, name="v_plane_list", align_bytes=64)
        v_plane = keep.tile([P, S], U8, name="v_plane", align_bytes=64)

        tab, wd_raw, x_raw, r_sb = {}, {}, {}, {}
        x_grouped, h_grouped, wd_picked, wd_grouped = {}, {}, {}, {}
        x_mx, h_mx, wd_mx = {}, {}, {}
        summed, squashed, gained_rows, last_banks = {}, {}, {}, {}


        def load_table(a):
            tab[a] = ring.tile([P, T], I32, name="table", align_bytes=64, bufs=TABLE_SLOTS)
            nc.sync.dma_start(tab[a][:], tab_words[a].rearrange("p t i -> p (t i)").bitcast(I32))

        def load_readout(i):
            wd_raw[i] = ring.tile([P, T], F32, name="table", align_bytes=64, bufs=TABLE_SLOTS)
            nc.sync.dma_start(wd_raw[i][:], wdT[i * P : (i + 1) * P, :])

        def load_rows(src, half, m0):
            rows = ring.tile([P, PACK, CHUNK], F32, name="rows", align_bytes=64, bufs=ROWS_SLOTS)
            part = src[half * PASS : (half + 1) * PASS, m0 : m0 + CHUNK]
            nc.sync.dma_start(rows[:], part.rearrange("(p t) m -> p t m", t=PACK))
            return rows

        def load_x(a, m0):
            x_raw[(a, m0)] = load_rows(x, a, m0)

        def load_r(b, m0):
            r_sb[(b, m0)] = load_rows(r, b, m0)

        def load_direct_words():
            nc.sync.dma_start(wf[:], wf_words.bitcast(I32).rearrange("a p e -> p a e"))

        def load_direct_scales(s):
            nc.sync.dma_start(wf_plane[s:P:32, :, :], wf_scales.bitcast(I32)[:, s:16:4, :].rearrange("a q e -> q a e"))

        def load_biases():
            nc.scalar.dma_start(vectors[2:3, :], c.rearrange("(o n) -> o n", o=1))

        def load_gains():
            nc.scalar.dma_start(vectors[0:2, :], g.rearrange("(b j) -> b j", b=2))

        def turn_biases():
            turned = bank_tile([P, N // P, P])
            for i in range(N // P):
                nc.tensor.transpose(turned[:, i, :], vectors[:, i * P : (i + 1) * P], ident[:])
            nc.scalar.copy(c_sb[:], turned[:, :, 2])

        def turn_gains():
            turned = bank_tile([P, PACK, P])
            for t in range(PACK):
                nc.tensor.transpose(turned[:, t, :], vectors[:, t:PASS:PACK], ident[:])
            nc.scalar.copy(g_sb[:], turned[:, :, 0:2].rearrange("p t b -> p b t"))
            nc.scalar.copy(
                g_wide[:].rearrange("p b (m t) -> p b m t", t=PACK),
                g_sb[:].rearrange("p b (o t) -> p b o t", o=1).to_broadcast([P, 2, GAIN_RUN, PACK]),
            )


        def gather_table_words(a):
            nc.vector.tensor_copy(
                v_codes[a][:].rearrange("k (b t p) -> k b p t", b=2, t=PACK),
                tab[a][:].bitcast(U32).indirect(offsets[:]),
            )

        def gather_table_scales():
            nc.vector.tensor_copy(v_plane_list[:], tab_plane[:].bitcast(U8).indirect(offsets[:]))

        def order_table_scales():
            nc.vector.tensor_copy(
                v_plane[:].rearrange("k (b t p) -> k b t p", b=2, t=PACK),
                v_plane_list[:].rearrange("k (b p t) -> k b t p", b=2, t=PACK),
            )


        def quantize(grouped, width):
            mx = vector_tile([P, 5 * width], U8)
            nc.vector.quantize_mx(out=mx[:, 0 : 4 * width].bitcast(FP8X4), scales=mx[:, 4 * width : 5 * width], in_=grouped)
            return mx, width

        def operand(quantized, first):
            mx, width = quantized
            return mx[:, 4 * first : 4 * (first + P)].bitcast(FP8X4), mx[:, 4 * width + first : 4 * width + first + P]

        def columns(tiles, half, m0):
            start = max(key[1] for key in tiles if key[0] == half and key[1] <= m0)
            return operand(tiles[(half, start)], m0 - start)

        def as_grouped(tile):
            return tile[:].rearrange("p (e i) t -> p e t i", i=4)

        def as_rows(tile):
            return tile[:].rearrange("p t (e i) -> p e t i", i=4)

        def group_x_on_scalar(a, m0):
            x_grouped[(a, m0)] = scalar_tile([P, CHUNK, PACK], BF16)
            nc.scalar.copy(as_grouped(x_grouped[(a, m0)]), as_rows(x_raw[(a, m0)]))

        def group_x_on_vector(a, m0):
            x_grouped[(a, m0)] = vector_tile([P, CHUNK, PACK], BF16)
            nc.vector.tensor_copy(as_grouped(x_grouped[(a, m0)]), as_rows(x_raw[(a, m0)]))

        def quantize_x(a, m0):
            x_mx[(a, m0)] = quantize(x_grouped[(a, m0)][:].rearrange("p m t -> p (m t)"), CHUNK)


        def project(b, m0):
            bank = bank_tile([P, PACK, P])
            for t in range(PACK):
                picks = slice(b * PASS + t * P, b * PASS + (t + 1) * P)
                for a in range(2):
                    codes, plane = columns(x_mx, a, m0)
                    nc.tensor.matmul_mx(
                        out=bank[:, t, :],
                        lhsT=v_codes[a][:, picks].bitcast(FP8X4),
                        lhsT_scale=v_plane[4 * a : P, picks],
                        rhs=codes,
                        rhs_scale=plane,
                        start=(a == 0),
                        stop=(a == 1),
                    )
            summed[(b, m0)] = vector_tile([P, PACK, P], F32)
            start = m0 // CHUNK * CHUNK
            drive = r_sb[(b, start)][:, :, m0 - start : m0 - start + P]
            nc.vector.tensor_tensor(summed[(b, m0)][:], bank[:], drive, ALU.add)


        def tanh_grouped(b, m0, width):
            squashed[(b, m0)] = scalar_tile([P, width // P, PACK * P], F32)
            for s in range(width // P):
                nc.scalar.activation(
                    squashed[(b, m0)][:, s, :].rearrange("p (e i t) -> p e t i", i=4, t=PACK),
                    as_rows(summed[(b, m0 + s * P)]),
                    ACT.Tanh,
                )

        def gain_on_vector(b, m0):
            h_grouped[(b, m0)] = vector_tile([P, P, PACK], BF16)
            nc.vector.tensor_tensor(
                h_grouped[(b, m0)][:],
                squashed[(b, m0)][:].rearrange("p s (m t) -> p (s m) t", t=PACK),
                g_sb[:, b : b + 1, :].to_broadcast([P, P, PACK]),
                ALU.mult,
            )

        def gain_on_gpsimd(b, m0):
            h_grouped[(b, m0)] = gpsimd_tile([P, CHUNK, PACK], BF16)
            nc.gpsimd.tensor_tensor(
                h_grouped[(b, m0)][:].rearrange("p (s m) t -> p s (m t)", m=GAIN_RUN),
                squashed[(b, m0)][:].rearrange("p s (h e) -> p (s h) e", e=GAIN_RUN * PACK),
                g_wide[:, b : b + 1, :].to_broadcast([P, CHUNK // GAIN_RUN, GAIN_RUN * PACK]),
                ALU.mult,
            )

        def tanh_by_rows(b, m0, width):
            squashed[(b, m0)] = scalar_tile([P, width // P, PACK * P], F32)
            for s in range(width // P):
                nc.scalar.activation(squashed[(b, m0)][:, s, :], summed[(b, m0 + s * P)][:].rearrange("p t m -> p (t m)"), ACT.Tanh)

        def gain_on_scalar(b, m0):
            gained_rows[(b, m0)] = scalar_tile([P, PACK, CHUNK], BF16)
            for t in range(PACK):
                nc.scalar.activation(
                    gained_rows[(b, m0)][:, t, :].rearrange("p (s m) -> p s m", m=P),
                    squashed[(b, m0)][:, :, t * P : (t + 1) * P],
                    ACT.Copy,
                    scale=g_sb[:, b, t : t + 1],
                )

        def group_h(b, m0):
            h_grouped[(b, m0)] = vector_tile([P, CHUNK, PACK], BF16)
            nc.vector.tensor_copy(as_grouped(h_grouped[(b, m0)]), as_rows(gained_rows[(b, m0)]))

        def quantize_h(b, m0):
            grouped = h_grouped[(b, m0)]
            h_mx[(b, m0)] = quantize(grouped[:].rearrange("p m t -> p (m t)"), grouped[:].shape[1])


        def gather_readout(i):
            wd_picked[i] = vector_tile([P, 2, PASS + PAD], BF16)
            nc.vector.tensor_copy(wd_picked[i][:, :, 0:PASS], wd_raw[i][:].indirect(offsets[:]))

        def turn_readout(i):
            turned = bank_tile([P, 4, P])
            for b in range(2):
                pairs = wd_picked[i][:, b, 0:PASS].bitcast(F32)
                for u in range(2):
                    nc.tensor.transpose(turned[:, 2 * b + u, :], pairs[:, u : 2 * P : 2], ident[:])
            wd_grouped[i] = scalar_tile([P, S], BF16)
            nc.scalar.copy(
                wd_grouped[i][:].bitcast(F32).rearrange("p (b n u) -> p b n u", b=2, u=2),
                turned[:].rearrange("p (b u) n -> p b n u", b=2),
            )

        def quantize_readout(i):
            wd_mx[i] = quantize(wd_grouped[i][:], 2 * P)


        def direct_passes(group, i, m0):
            for a in range(2):
                codes, plane = columns(x_mx, a, m0)
                nc.tensor.matmul_mx(
                    out=group,
                    lhsT=wf[:, a, :].bitcast(U8)[:, 2 * i * P : 2 * (i + 1) * P].bitcast(FP4X4),
                    lhsT_scale=wf_plane[:, a, :].bitcast(U8)[:, i * P : (i + 1) * P],
                    rhs=codes,
                    rhs_scale=plane,
                    start=(a == 0),
                    stop=False,
                )

        def readout_passes(group, i, m0):
            for b in range(2):
                codes, plane = columns(h_mx, b, m0)
                weights, weight_plane = operand(wd_mx[i], b * P)
                nc.tensor.matmul_mx(
                    out=group,
                    lhsT=weights,
                    lhsT_scale=weight_plane,
                    rhs=codes,
                    rhs_scale=plane,
                    start=False,
                    stop=(b == 1),
                )

        def saturate_and_store(bank, i, m0, groups):
            result = scalar_tile([P, groups * P], F32)
            nc.scalar.activation(result[:], bank[:].rearrange("p s w -> p (s w)"), ACT.Tanh, bias=c_sb[:, i : i + 1])
            nc.sync.dma_start(out[i * P : (i + 1) * P, m0 : m0 + groups * P], result[:])

        def commands(i, m0, groups):
            bank = bank_tile([P, groups, P])
            for s in range(groups):
                direct_passes(bank[:, s, :], i, m0 + s * P)
                readout_passes(bank[:, s, :], i, m0 + s * P)
            saturate_and_store(bank, i, m0, groups)


        def open_last_commands(i):
            last_banks[i] = bank_tile([P, 1, P])
            direct_passes(last_banks[i][:, 0, :], i, LAST)

        def close_last_commands(i):
            readout_passes(last_banks[i][:, 0, :], i, LAST)
            saturate_and_store(last_banks[i], i, LAST, 1)


        load_x(0, 0)
        load_table(1)
        group_x_on_scalar(0, 0)
        load_x(1, 0)
        gather_table_scales()
        load_table(0)
        group_x_on_scalar(1, 0)
        load_x(1, 256)
        load_biases()
        load_x(0, 256)
        quantize_x(0, 0)
        load_r(1, 0)
        group_x_on_scalar(1, 256)
        quantize_x(1, 256)
        quantize_x(1, 0)
        load_r(0, 0)
        load_readout(0)
        load_r(1, 256)
        load_gains()
        order_table_scales()
        turn_biases()
        group_x_on_vector(0, 256)
        gather_table_words(0)
        turn_gains()
        gather_table_words(1)
        load_x(0, 512)
        quantize_x(0, 256)
        load_r(0, 256)
        load_readout(1)
        load_direct_scales(1)
        load_direct_scales(0)

        project(0, 0)
        project(1, 0)
        project(1, 128)
        tanh_by_rows(1, 0, 256)
        project(0, 128)
        tanh_grouped(0, 0, 256)
        load_x(1, 512)
        gain_on_scalar(1, 0)
        gather_readout(0)
        group_x_on_scalar(0, 512)
        project(1, 256)
        load_direct_scales(3)
        project(1, 384)
        project(0, 384)
        load_readout(2)
        project(0, 256)
        turn_readout(0)
        group_x_on_scalar(1, 512)
        load_r(1, 512)
        load_direct_scales(2)
        group_h(1, 0)
        tanh_grouped(1, 256, 256)
        gather_readout(1)
        quantize_x(0, 512)
        load_x(0, 768)
        quantize_readout(0)
        load_r(0, 512)
        load_direct_words()
        quantize_h(1, 0)
        quantize_x(1, 512)
        gain_on_gpsimd(0, 0)
        quantize_h(0, 0)

        gather_readout(2)
        project(1, 640)
        tanh_by_rows(0, 256, 256)
        gain_on_scalar(0, 256)
        project(1, 512)
        gain_on_gpsimd(1, 256)
        project(0, 512)
        project(0, 640)
        load_x(1, 768)
        group_h(0, 256)
        turn_readout(1)
        quantize_readout(1)
        group_x_on_scalar(0, 768)
        load_readout(3)
        quantize_x(0, 768)
        turn_readout(2)
        quantize_h(1, 256)
        group_x_on_scalar(1, 768)
        load_r(1, 768)
        tanh_grouped(1, 512, 256)
        quantize_h(0, 256)
        tanh_by_rows(0, 512, 256)
        quantize_readout(2)

        commands(0, 0, 4)
        quantize_x(1, 768)
        gain_on_gpsimd(1, 512)
        gather_readout(3)
        commands(1, 0, 4)
        project(1, 896)
        gain_on_scalar(0, 512)
        load_r(0, 768)
        project(0, 896)
        project(0, 768)
        project(1, 768)
        turn_readout(3)
        quantize_readout(3)

        tanh_grouped(0, 768, 128)
        tanh_grouped(1, 768, 128)
        group_h(0, 512)
        tanh_grouped(0, 896, 128)
        quantize_h(1, 512)
        quantize_h(0, 512)
        tanh_grouped(1, 896, 128)
        gain_on_vector(0, 768)
        commands(3, 0, 4)
        gain_on_vector(1, 768)
        commands(2, 0, 4)
        open_last_commands(0)
        quantize_h(0, 768)
        quantize_h(1, 768)
        gain_on_vector(1, 896)
        commands(0, 512, 3)
        gain_on_vector(0, 896)
        commands(1, 512, 3)
        quantize_h(1, 896)
        commands(2, 512, 3)
        quantize_h(0, 896)
        commands(3, 512, 3)
        open_last_commands(2)
        open_last_commands(3)
        open_last_commands(1)
        close_last_commands(1)
        close_last_commands(2)
        close_last_commands(0)
        close_last_commands(3)
